import numpy as np
import ml_dtypes


def mxq(x, axis, fmt="e4m3"):
    dtype, down = {"e4m3": (ml_dtypes.float8_e4m3fn, 7), "e5m2": (ml_dtypes.float8_e5m2, 14)}[fmt]
    v = np.moveaxis(np.asarray(x, np.float32).astype(ml_dtypes.bfloat16).astype(np.float64), axis, -1)
    blocks = v.reshape(v.shape[:-1] + (-1, 32))
    amax = np.abs(blocks).max(-1, keepdims=True)
    byte = np.maximum(np.where(amax > 0, np.frexp(amax)[1] - 1 + 127, 0) - down, 1)
    scale = np.exp2(byte - 127.0)
    codes = (blocks / scale).astype(np.float32).astype(dtype).astype(np.float64)
    return np.moveaxis((codes * scale).reshape(v.shape), -1, axis)


WIDE = False


def mx_kscale(k):
    if not WIDE:
        return np.ones(k)
    levels = np.array([24, -24, 12, -12, 0])
    if k % 512:
        return np.exp2(np.random.permutation(np.resize(levels, k // 32))).repeat(32)
    a = np.empty((k // 512, 16))
    for p in range(k // 512):
        a[p, :8] = np.random.permutation(np.resize(levels, 8))
        for g in range(8):
            far = levels[np.abs(levels - a[p, g]) >= 10]
            a[p, g + 8] = far[np.random.randint(len(far))]
    return np.exp2(a.ravel()).repeat(32)


def f64(x):
    return np.asarray(x).astype(np.float64)


def striped8(idx):
    return np.concatenate([v.reshape(-1, 16).T for v in idx]).astype(np.uint16)


def unstriped8(offs):
    return np.stack([offs[16 * g:16 * g + 16].T.reshape(-1) for g in range(8)]).astype(np.int64)


E2M1 = np.array([0.0, 0.5, 1.0, 1.5, 2.0, 3.0, 4.0, 6.0, -0.0, -0.5, -1.0, -1.5, -2.0, -3.0, -4.0, -6.0])


def pack_weight(w, fmt):
    k, n = w.shape
    w = f64(np.asarray(w, np.float32).astype(ml_dtypes.bfloat16)).reshape(k // 32, 32, n)
    amax = np.abs(w).max(1)
    if fmt == "e4m3":
        byte = np.frexp(amax)[1] - 1 + 127 - 7
    else:
        mant, ex = np.frexp(amax / 6.0)
        byte = np.where(mant > 0.5, ex, ex - 1) + 127
    byte = np.clip(np.where(amax > 0, byte, 1), 1, 254)
    scaled = (w * np.exp2(127.0 - byte)[:, None, :]).reshape(k, n).astype(np.float32)
    by_word = np.ascontiguousarray(scaled.reshape(k // 512, 128, 4, n).transpose(0, 1, 3, 2))
    if fmt == "e4m3":
        words = by_word.astype(ml_dtypes.float8_e4m3fn).view(np.uint8)
    else:
        c = by_word.astype(ml_dtypes.float4_e2m1fn).view(np.uint8) & 0xF
        words = (c[..., 0::2] | (c[..., 1::2] << 4)).reshape(k // 512, 128, 2 * n)
    return np.ascontiguousarray(words), np.ascontiguousarray(byte.astype(np.uint8).reshape(k // 512, 16, n))


def unpack_weight(words, scales, fmt):
    g, _, n = scales.shape
    words = np.ascontiguousarray(words).reshape(g, 128, n, -1)
    if fmt == "e4m3":
        vals = words.view(ml_dtypes.float8_e4m3fn).astype(np.float64)
    else:
        nib = np.empty((g, 128, n, 4), np.uint8)
        nib[..., 0::2] = words & 0xF
        nib[..., 1::2] = words >> 4
        vals = E2M1[nib]
    vals = vals * np.repeat(np.exp2(scales.astype(np.float64) - 127.0), 8, axis=1)[..., None]
    return vals.transpose(0, 1, 3, 2).reshape(g * 512, n)


def planes(y):
    n, m = y.shape
    v = y.astype(np.float32).astype(ml_dtypes.bfloat16).astype(np.float64).reshape(n // 32, 32, m)
    top = np.abs(v).max(1)
    byte = np.clip(np.where(top > 0, np.frexp(top)[1] - 1 + 127 - 7, 1), 1, 254)
    codes = (v * np.exp2(127.0 - byte)[:, None, :]).reshape(n, m).astype(np.float32).astype(ml_dtypes.float8_e4m3fn).view(np.uint8)
    words = codes.reshape(n // 512, 128, 4, m).transpose(0, 1, 3, 2)
    return np.ascontiguousarray(words), np.ascontiguousarray(byte.astype(np.uint8).reshape(n // 512, 16, m))


K, N, T, J = 512, 512, 2048, 512


def setup_inputs():
    n = np.random.standard_normal
    s = mx_kscale(K)[:, None]
    p_w = pack_weight(n((K, N)) / np.sqrt(K) / s, "e2m1")
    return {
        "xT": (n((K, T)) * s).astype(np.float32),
        "wgt": np.repeat(np.random.uniform(0.5, 2.0, (8, 2 * J)), 16, axis=0).astype(np.float32),
        "w_words": p_w[0],
        "w_scales": p_w[1],
        "offs": striped8(np.stack([np.concatenate([np.random.permutation(T)[:J] for _ in range(2)]) for _ in range(8)])),
    }


def reference(xT, wgt, w_words, w_scales, offs):
    idx = unstriped8(offs)
    rows = np.arange(K)
    xg = f64(wgt)[rows // 4 % 128] * f64(xT)[rows[:, None], idx[rows % 512 // 64]]
    xT_ = mxq(xg, 0, "e4m3").reshape(K, 2, J)
    w_ = unpack_weight(w_words, w_scales, "e2m1")
    a0 = w_.T @ xT_[:, 0]
    a1 = w_.T @ xT_[:, 1]
    out_0 = np.abs(a0 - a1)
    return (out_0,) + planes(out_0)

@@ -1,0 +1,120 @@
+from contextlib import ExitStack
+
+import concourse.mybir as mybir
+
+K, N, T, J = 512, 512, 2048, 512
+FLOPS = 2 * 2 * K * N * J
+
+F32 = mybir.dt.float32
+BF16 = mybir.dt.bfloat16
+I32 = mybir.dt.int32
+U32 = mybir.dt.uint32
+U16 = mybir.dt.uint16
+U8 = mybir.dt.uint8
+FP8X4 = mybir.dt.float8_e4m3fn_x4
+FP4X4 = mybir.dt.float4_e2m1fn_x4
+MULT = mybir.AluOpType.mult
+COPY = mybir.ActivationFunctionType.Copy
+ABS = mybir.ActivationFunctionType.Abs
+
+P = 128
+PACK = 4
+PICKS = 2
+CH = 128
+NCH = J // CH
+LIST_ROWS = 16
+
+
+def tile_list_span_noneP_kernel(tc, xT, wgt, w_words, w_scales, offs, out_0, out_1, out_2):
+    nc = tc.nc
+    with ExitStack() as ctx:
+        keep = ctx.enter_context(tc.tile_pool(name="keep", bufs=1))
+        ring = ctx.enter_context(tc.tile_pool(name="ring", bufs=2))
+        psum = ctx.enter_context(tc.psum_pool(name="psum", bufs=1))
+
+        offsets = keep.tile([P, PICKS * J // LIST_ROWS], U16, name="offsets")
+        nc.sync.dma_start(offsets[:], offs)
+
+        w_raw = keep.tile([P, 2 * N], U8, name="w_raw", align_bytes=64)
+        ws_raw = keep.tile([P, N], U8, name="ws_raw", align_bytes=64)
+        nc.vector.memset(ws_raw[:].bitcast(I32), 0)
+        nc.scalar.dma_start(out=w_raw[:].bitcast(I32), in_=w_words[0].bitcast(I32))
+        for q in range(4):
+            nc.scalar.dma_start(out=ws_raw[32 * q : 32 * q + 4, :].bitcast(I32), in_=w_scales[0, 4 * q : 4 * q + 4, :].bitcast(I32))
+
+        x_rows = xT.rearrange("(p i) t -> p i t", i=PACK)
+        wg = [keep.tile([P, J], F32, name=f"wg{c}") for c in range(PICKS)]
+        xs = [keep.tile([P, T], F32, name=f"x{i}") for i in range(PACK)]
+        nc.sync.dma_start(out=wg[0][:], in_=wgt[:, 0:J])
+        nc.sync.dma_start(out=xs[0][:], in_=x_rows[:, 0, :])
+        nc.sync.dma_start(out=wg[1][:], in_=wgt[:, J : 2 * J])
+        for i in range(1, PACK):
+            nc.sync.dma_start(out=xs[i][:], in_=x_rows[:, i, :])
+
+        w_codes = keep.tile([P, 2 * N], U8, name="w_codes", align_bytes=64)
+        w_sc = keep.tile([P, N], U8, name="w_sc", align_bytes=64)
+        nc.vector.tensor_copy(
+            out=w_codes[:].rearrange("p (t m b) -> p t m b", t=PACK, b=2),
+            in_=w_raw[:].rearrange("p (m t b) -> p t m b", t=PACK, b=2),
+        )
+        nc.vector.tensor_copy(
+            out=w_sc[:].rearrange("p (t m) -> p t m", t=PACK),
+            in_=ws_raw[:].rearrange("p (m t) -> p t m", t=PACK),
+        )
+
+        wneg = keep.tile([P, J], F32, name="wneg")
+        nc.scalar.activation(out=wneg[:], in_=wg[1][:], func=COPY, scale=-1.0)
+        signed = [wg[0], wneg]
+
+        def gather(dst, i, c, j0, width):
+            a = (c * J + j0) // LIST_ROWS
+            nc.vector.tensor_tensor(dst, xs[i][:].indirect(offsets[:, a : a + width // LIST_ROWS]), signed[c][:, j0 : j0 + width], MULT)
+
+        g01 = keep.tile([P, 2, PICKS, J], F32, name="g01")
+        for i in range(2):
+            for c in range(PICKS):
+                gather(g01[:, i, c, :], i, c, 0, J)
+
+        packed = [keep.tile([P, PICKS, CH, PACK], BF16, name=f"packed{q}", align_bytes=64) for q in range(NCH)]
+        for q in range(NCH):
+            nc.scalar.copy(out=packed[q][:, :, :, 0:2], in_=g01[:, :, :, q * CH : (q + 1) * CH].rearrange("p i c j -> p c j i"))
+
+        o_codes = keep.tile([P, J], U32, name="o_codes", align_bytes=64)
+        o_sc = keep.tile([P, J], U8, name="o_sc", align_bytes=64)
+        y_rows = out_0.rearrange("(p t) j -> p t j", t=PACK)
+        o_words = out_1[0].rearrange("p j i -> p (j i)").bitcast(I32)
+
+        for q in range(NCH):
+            cols = slice(q * CH, (q + 1) * CH)
+            g23 = ring.tile([P, 2, PICKS, CH], F32, name="g23")
+            for i in range(2):
+                for c in range(PICKS):
+                    gather(g23[:, i, c, :], 2 + i, c, q * CH, CH)
+            nc.scalar.copy(out=packed[q][:, :, :, 2:4], in_=g23[:].rearrange("p i c j -> p c j i"))
+            x_codes = keep.tile([P, PICKS * CH], U32, name=f"x_codes{q}", align_bytes=64)
+            x_sc = keep.tile([P, PICKS * CH], U8, name=f"x_sc{q}", align_bytes=64)
+            nc.vector.quantize_mx(out=x_codes[:].bitcast(FP8X4), scales=x_sc[:], in_=packed[q][:].rearrange("p c j i -> p (c j i)"))
+            acc = psum.tile([P, PACK, CH], F32, name=f"acc{q}")
+            for t in range(PACK):
+                for c in range(PICKS):
+                    nc.tensor.matmul_mx(
+                        out=acc[:, t, :],
+                        lhsT=w_codes[:, 2 * P * t : 2 * P * (t + 1)].bitcast(FP4X4),
+                        lhsT_scale=w_sc[:, P * t : P * (t + 1)],
+                        rhs=x_codes[:, c * CH : (c + 1) * CH].bitcast(FP8X4),
+                        rhs_scale=x_sc[:, c * CH : (c + 1) * CH],
+                        start=(c == 0),
+                        stop=(c == PICKS - 1),
+                    )
+            y_packed = keep.tile([P, CH, PACK], BF16, name=f"y_packed{q}", align_bytes=64)
+            nc.scalar.activation(out=y_packed[:], in_=acc[:].rearrange("p t j -> p j t"), func=ABS)
+            y = keep.tile([P, PACK, CH], F32, name=f"y{q}")
+            nc.scalar.activation(out=y[:], in_=acc[:], func=ABS)
+            nc.sync.dma_start(out=y_rows[:, :, cols], in_=y[:])
+            nc.vector.quantize_mx(out=o_codes[:, cols].bitcast(FP8X4), scales=o_sc[:, cols], in_=y_packed[:].rearrange("p j t -> p (j t)"))
+            if q % 2 == 1:
+                half = slice((q - 1) * CH, (q + 1) * CH)
+                nc.sync.dma_start(out=o_words[:, half], in_=o_codes[:, half].bitcast(I32))
+        for q in range(4):
+            eng = nc.sync if q < 2 else nc.scalar
+            eng.dma_start(out=out_2[0, 4 * q : 4 * q + 4, :].bitcast(I32), in_=o_sc[32 * q : 32 * q + 4, :].bitcast(I32))

@@ -29,23 +29,22 @@ def tile_list_span_noneP_kernel(tc, xT, wgt, w_words, w_scales, offs, out_0, out
     nc = tc.nc
     with ExitStack() as ctx:
         keep = ctx.enter_context(tc.tile_pool(name="keep", bufs=1))
-        ring = ctx.enter_context(tc.tile_pool(name="ring", bufs=2))
+        ring = ctx.enter_context(tc.tile_pool(name="ring", bufs=3))
         psum = ctx.enter_context(tc.psum_pool(name="psum", bufs=1))
 
+        ws_raw = keep.tile([P, N], U8, name="ws_raw", align_bytes=64)
+        nc.gpsimd.memset(ws_raw[:].bitcast(I32), 0)
         offsets = keep.tile([P, PICKS * J // LIST_ROWS], U16, name="offsets")
         nc.sync.dma_start(offsets[:], offs)
 
         w_raw = keep.tile([P, 2 * N], U8, name="w_raw", align_bytes=64)
-        ws_raw = keep.tile([P, N], U8, name="ws_raw", align_bytes=64)
-        nc.vector.memset(ws_raw[:].bitcast(I32), 0)
-        nc.scalar.dma_start(out=w_raw[:].bitcast(I32), in_=w_words[0].bitcast(I32))
-        for q in range(4):
-            nc.scalar.dma_start(out=ws_raw[32 * q : 32 * q + 4, :].bitcast(I32), in_=w_scales[0, 4 * q : 4 * q + 4, :].bitcast(I32))
-
         x_rows = xT.rearrange("(p i) t -> p i t", i=PACK)
         wg = [keep.tile([P, J], F32, name=f"wg{c}") for c in range(PICKS)]
         xs = [keep.tile([P, T], F32, name=f"x{i}") for i in range(PACK)]
+        nc.sync.dma_start(out=w_raw[:].bitcast(I32), in_=w_words[0].bitcast(I32))
         nc.sync.dma_start(out=wg[0][:], in_=wgt[:, 0:J])
+        for q in range(4):
+            nc.sync.dma_start(out=ws_raw[32 * q : 32 * q + 4, :].bitcast(I32), in_=w_scales[0, 4 * q : 4 * q + 4, :].bitcast(I32))
         nc.sync.dma_start(out=xs[0][:], in_=x_rows[:, 0, :])
         nc.sync.dma_start(out=wg[1][:], in_=wgt[:, J : 2 * J])
         for i in range(1, PACK):
@@ -63,21 +62,25 @@ def tile_list_span_noneP_kernel(tc, xT, wgt, w_words, w_scales, offs, out_0, out
         )
 
         wneg = keep.tile([P, J], F32, name="wneg")
-        nc.scalar.activation(out=wneg[:], in_=wg[1][:], func=COPY, scale=-1.0)
-        signed = [wg[0], wneg]
+        nc.scalar.activation(out=wneg[:], in_=wg[0][:], func=COPY, scale=-1.0)
+        signed = [wneg, wg[1]]
 
         def gather(dst, i, c, j0, width):
             a = (c * J + j0) // LIST_ROWS
             nc.vector.tensor_tensor(dst, xs[i][:].indirect(offsets[:, a : a + width // LIST_ROWS]), signed[c][:, j0 : j0 + width], MULT)
 
-        g01 = keep.tile([P, 2, PICKS, J], F32, name="g01")
-        for i in range(2):
+        HALF = J // 2
+        g01 = [keep.tile([P, 2, PICKS, HALF], F32, name=f"g01_{h}") for h in range(2)]
+        for c in range(PICKS):
+            for h in range(2):
+                gather(g01[h][:, 0, c, :], 0, c, h * HALF, HALF)
+        for h in range(2):
             for c in range(PICKS):
-                gather(g01[:, i, c, :], i, c, 0, J)
+                gather(g01[h][:, 1, c, :], 1, c, h * HALF, HALF)
 
         packed = [keep.tile([P, PICKS, CH, PACK], BF16, name=f"packed{q}", align_bytes=64) for q in range(NCH)]
         for q in range(NCH):
-            nc.scalar.copy(out=packed[q][:, :, :, 0:2], in_=g01[:, :, :, q * CH : (q + 1) * CH].rearrange("p i c j -> p c j i"))
+            nc.scalar.copy(out=packed[q][:, :, :, 0:2], in_=g01[q // 2][:, :, :, (q % 2) * CH : (q % 2 + 1) * CH].rearrange("p i c j -> p c j i"))
 
         o_codes = keep.tile([P, J], U32, name="o_codes", align_bytes=64)
         o_sc = keep.tile([P, J], U8, name="o_sc", align_bytes=64)
@@ -86,30 +89,52 @@ def tile_list_span_noneP_kernel(tc, xT, wgt, w_words, w_scales, offs, out_0, out
 
         for q in range(NCH):
             cols = slice(q * CH, (q + 1) * CH)
-            g23 = ring.tile([P, 2, PICKS, CH], F32, name="g23")
-            for i in range(2):
-                for c in range(PICKS):
-                    gather(g23[:, i, c, :], 2 + i, c, q * CH, CH)
-            nc.scalar.copy(out=packed[q][:, :, :, 2:4], in_=g23[:].rearrange("p i c j -> p c j i"))
+            g23 = ring.tile([P, PICKS, 2, CH], F32, name="g23")
             x_codes = keep.tile([P, PICKS * CH], U32, name=f"x_codes{q}", align_bytes=64)
             x_sc = keep.tile([P, PICKS * CH], U8, name=f"x_sc{q}", align_bytes=64)
-            nc.vector.quantize_mx(out=x_codes[:].bitcast(FP8X4), scales=x_sc[:], in_=packed[q][:].rearrange("p c j i -> p (c j i)"))
             acc = psum.tile([P, PACK, CH], F32, name=f"acc{q}")
-            for t in range(PACK):
+
+            def project(c, t, start, stop):
+                nc.tensor.matmul_mx(
+                    out=acc[:, t, :],
+                    lhsT=w_codes[:, 2 * P * t : 2 * P * (t + 1)].bitcast(FP4X4),
+                    lhsT_scale=w_sc[:, P * t : P * (t + 1)],
+                    rhs=x_codes[:, c * CH : (c + 1) * CH].bitcast(FP8X4),
+                    rhs_scale=x_sc[:, c * CH : (c + 1) * CH],
+                    start=start,
+                    stop=stop,
+                )
+
+            if q < NCH - 1:
+                for i in range(2):
+                    for c in range(PICKS):
+                        gather(g23[:, c, i, :], 2 + i, c, q * CH, CH)
+                nc.scalar.copy(out=packed[q][:, :, :, 2:4], in_=g23[:].rearrange("p c i j -> p c j i"))
+                nc.vector.quantize_mx(out=x_codes[:].bitcast(FP8X4), scales=x_sc[:], in_=packed[q][:].rearrange("p c j i -> p (c j i)"))
+                for t in range(PACK):
+                    for c in range(PICKS):
+                        project(c, t, c == 0, c == PICKS - 1)
+            else:
                 for c in range(PICKS):
-                    nc.tensor.matmul_mx(
-                        out=acc[:, t, :],
-                        lhsT=w_codes[:, 2 * P * t : 2 * P * (t + 1)].bitcast(FP4X4),
-                        lhsT_scale=w_sc[:, P * t : P * (t + 1)],
-                        rhs=x_codes[:, c * CH : (c + 1) * CH].bitcast(FP8X4),
-                        rhs_scale=x_sc[:, c * CH : (c + 1) * CH],
-                        start=(c == 0),
-                        stop=(c == PICKS - 1),
-                    )
+                    for i in range(2):
+                        gather(g23[:, c, i, :], 2 + i, c, q * CH, CH)
+                    src = g23[:, c].rearrange("p i j -> p j i")
+                    if c in (1,):
+                        nc.vector.tensor_copy(out=packed[q][:, c, :, 2:4], in_=src)
+                    else:
+                        nc.scalar.copy(out=packed[q][:, c, :, 2:4], in_=src)
+                    pick = slice(c * CH, (c + 1) * CH)
+                    nc.vector.quantize_mx(out=x_codes[:, pick].bitcast(FP8X4), scales=x_sc[:, pick], in_=packed[q][:, c].rearrange("p j i -> p (j i)"))
+                    for t in range(PACK):
+                        project(c, t, c == 0 and t == 0, c == PICKS - 1 and t == PACK - 1)
             y_packed = keep.tile([P, CH, PACK], BF16, name=f"y_packed{q}", align_bytes=64)
-            nc.scalar.activation(out=y_packed[:], in_=acc[:].rearrange("p t j -> p j t"), func=ABS)
             y = keep.tile([P, PACK, CH], F32, name=f"y{q}")
-            nc.scalar.activation(out=y[:], in_=acc[:], func=ABS)
+            if q in (1, 2):
+                nc.scalar.activation(out=y[:], in_=acc[:], func=ABS)
+                nc.vector.tensor_copy(out=y_packed[:], in_=y[:].rearrange("p t j -> p j t"))
+            else:
+                nc.scalar.activation(out=y_packed[:], in_=acc[:].rearrange("p t j -> p j t"), func=ABS)
+                nc.scalar.activation(out=y[:], in_=acc[:], func=ABS)
             nc.sync.dma_start(out=y_rows[:, :, cols], in_=y[:])
             nc.vector.quantize_mx(out=o_codes[:, cols].bitcast(FP8X4), scales=o_sc[:, cols], in_=y_packed[:].rearrange("p j t -> p (j t)"))
             if q % 2 == 1:

@@ -29,7 +29,7 @@ def tile_list_span_noneP_kernel(tc, xT, wgt, w_words, w_scales, offs, out_0, out
     nc = tc.nc
     with ExitStack() as ctx:
         keep = ctx.enter_context(tc.tile_pool(name="keep", bufs=1))
-        ring = ctx.enter_context(tc.tile_pool(name="ring", bufs=3))
+        ring = ctx.enter_context(tc.tile_pool(name="ring", bufs=5))
         psum = ctx.enter_context(tc.psum_pool(name="psum", bufs=1))
 
         ws_raw = keep.tile([P, N], U8, name="ws_raw", align_bytes=64)
@@ -87,16 +87,15 @@ def tile_list_span_noneP_kernel(tc, xT, wgt, w_words, w_scales, offs, out_0, out
         y_rows = out_0.rearrange("(p t) j -> p t j", t=PACK)
         o_words = out_1[0].rearrange("p j i -> p (j i)").bitcast(I32)
 
-        for q in range(NCH):
-            cols = slice(q * CH, (q + 1) * CH)
-            g23 = ring.tile([P, PICKS, 2, CH], F32, name="g23")
+        accs = [psum.tile([P, PACK, CH], F32, name=f"acc{q}") for q in range(NCH)]
+
+        def front(q):
             x_codes = keep.tile([P, PICKS * CH], U32, name=f"x_codes{q}", align_bytes=64)
             x_sc = keep.tile([P, PICKS * CH], U8, name=f"x_sc{q}", align_bytes=64)
-            acc = psum.tile([P, PACK, CH], F32, name=f"acc{q}")
 
             def project(c, t, start, stop):
                 nc.tensor.matmul_mx(
-                    out=acc[:, t, :],
+                    out=accs[q][:, t, :],
                     lhsT=w_codes[:, 2 * P * t : 2 * P * (t + 1)].bitcast(FP4X4),
                     lhsT_scale=w_sc[:, P * t : P * (t + 1)],
                     rhs=x_codes[:, c * CH : (c + 1) * CH].bitcast(FP8X4),
@@ -105,21 +104,26 @@ def tile_list_span_noneP_kernel(tc, xT, wgt, w_words, w_scales, offs, out_0, out
                     stop=stop,
                 )
 
-            if q < NCH - 1:
+            if q not in (0, 1, 2, 3):
                 for i in range(2):
                     for c in range(PICKS):
                         gather(g23[:, c, i, :], 2 + i, c, q * CH, CH)
-                nc.scalar.copy(out=packed[q][:, :, :, 2:4], in_=g23[:].rearrange("p c i j -> p c j i"))
+                src = g23[:].rearrange("p c i j -> p c j i")
+                if 2 * q + 1 in (7,):
+                    nc.vector.tensor_copy(out=packed[q][:, :, :, 2:4], in_=src)
+                else:
+                    nc.scalar.copy(out=packed[q][:, :, :, 2:4], in_=src)
                 nc.vector.quantize_mx(out=x_codes[:].bitcast(FP8X4), scales=x_sc[:], in_=packed[q][:].rearrange("p c j i -> p (c j i)"))
                 for t in range(PACK):
                     for c in range(PICKS):
                         project(c, t, c == 0, c == PICKS - 1)
             else:
                 for c in range(PICKS):
+                    g23 = ring.tile([P, 2, CH], F32, name="g23")
                     for i in range(2):
-                        gather(g23[:, c, i, :], 2 + i, c, q * CH, CH)
-                    src = g23[:, c].rearrange("p i j -> p j i")
-                    if c in (1,):
+                        gather(g23[:, i, :], 2 + i, c, q * CH, CH)
+                    src = g23[:].rearrange("p i j -> p j i")
+                    if 2 * q + c in (7,):
                         nc.vector.tensor_copy(out=packed[q][:, c, :, 2:4], in_=src)
                     else:
                         nc.scalar.copy(out=packed[q][:, c, :, 2:4], in_=src)
@@ -127,19 +131,29 @@ def tile_list_span_noneP_kernel(tc, xT, wgt, w_words, w_scales, offs, out_0, out
                     nc.vector.quantize_mx(out=x_codes[:, pick].bitcast(FP8X4), scales=x_sc[:, pick], in_=packed[q][:, c].rearrange("p j i -> p (j i)"))
                     for t in range(PACK):
                         project(c, t, c == 0 and t == 0, c == PICKS - 1 and t == PACK - 1)
+
+        def back(q):
+            cols = slice(q * CH, (q + 1) * CH)
             y_packed = keep.tile([P, CH, PACK], BF16, name=f"y_packed{q}", align_bytes=64)
             y = keep.tile([P, PACK, CH], F32, name=f"y{q}")
-            if q in (1, 2):
-                nc.scalar.activation(out=y[:], in_=acc[:], func=ABS)
+            if q in (0, 1, 2, 3):
+                nc.scalar.activation(out=y[:], in_=accs[q][:], func=ABS)
                 nc.vector.tensor_copy(out=y_packed[:], in_=y[:].rearrange("p t j -> p j t"))
             else:
-                nc.scalar.activation(out=y_packed[:], in_=acc[:].rearrange("p t j -> p j t"), func=ABS)
-                nc.scalar.activation(out=y[:], in_=acc[:], func=ABS)
+                nc.scalar.activation(out=y_packed[:], in_=accs[q][:].rearrange("p t j -> p j t"), func=ABS)
+                nc.scalar.activation(out=y[:], in_=accs[q][:], func=ABS)
             nc.sync.dma_start(out=y_rows[:, :, cols], in_=y[:])
             nc.vector.quantize_mx(out=o_codes[:, cols].bitcast(FP8X4), scales=o_sc[:, cols], in_=y_packed[:].rearrange("p j t -> p (j t)"))
             if q % 2 == 1:
-                half = slice((q - 1) * CH, (q + 1) * CH)
-                nc.sync.dma_start(out=o_words[:, half], in_=o_codes[:, half].bitcast(I32))
+                done = slice((q - 1) * CH, (q + 1) * CH)
+                nc.sync.dma_start(out=o_words[:, done], in_=o_codes[:, done].bitcast(I32))
+
+        LAG = 2
+        for q in range(NCH + LAG):
+            if q < NCH:
+                front(q)
+            if q >= LAG:
+                back(q - LAG)
         for q in range(4):
             eng = nc.sync if q < 2 else nc.scalar
             eng.dma_start(out=out_2[0, 4 * q : 4 * q + 4, :].bitcast(I32), in_=o_sc[32 * q : 32 * q + 4, :].bitcast(I32))

@@ -29,7 +29,6 @@ def tile_list_span_noneP_kernel(tc, xT, wgt, w_words, w_scales, offs, out_0, out
     nc = tc.nc
     with ExitStack() as ctx:
         keep = ctx.enter_context(tc.tile_pool(name="keep", bufs=1))
-        ring = ctx.enter_context(tc.tile_pool(name="ring", bufs=5))
         psum = ctx.enter_context(tc.psum_pool(name="psum", bufs=1))
 
         ws_raw = keep.tile([P, N], U8, name="ws_raw", align_bytes=64)
@@ -47,7 +46,7 @@ def tile_list_span_noneP_kernel(tc, xT, wgt, w_words, w_scales, offs, out_0, out
             nc.sync.dma_start(out=ws_raw[32 * q : 32 * q + 4, :].bitcast(I32), in_=w_scales[0, 4 * q : 4 * q + 4, :].bitcast(I32))
         nc.sync.dma_start(out=xs[0][:], in_=x_rows[:, 0, :])
         nc.sync.dma_start(out=wg[1][:], in_=wgt[:, J : 2 * J])
-        for i in range(1, PACK):
+        for i in (1, 3, 2):
             nc.sync.dma_start(out=xs[i][:], in_=x_rows[:, i, :])
 
         w_codes = keep.tile([P, 2 * N], U8, name="w_codes", align_bytes=64)
@@ -82,6 +81,11 @@ def tile_list_span_noneP_kernel(tc, xT, wgt, w_words, w_scales, offs, out_0, out
         for q in range(NCH):
             nc.scalar.copy(out=packed[q][:, :, :, 0:2], in_=g01[q // 2][:, :, :, (q % 2) * CH : (q % 2 + 1) * CH].rearrange("p i c j -> p c j i"))
 
+        AHEAD = 2
+        g23 = [keep.tile([P, (AHEAD + NCH) * CH], F32, name=f"g23_{c}") for c in range(PICKS)]
+        for c in range(PICKS):
+            gather(g23[c][:, AHEAD * CH :], 3, c, 0, J)
+
         o_codes = keep.tile([P, J], U32, name="o_codes", align_bytes=64)
         o_sc = keep.tile([P, J], U8, name="o_sc", align_bytes=64)
         y_rows = out_0.rearrange("(p t) j -> p t j", t=PACK)
@@ -104,44 +108,24 @@ def tile_list_span_noneP_kernel(tc, xT, wgt, w_words, w_scales, offs, out_0, out
                     stop=stop,
                 )
 
-            if q not in (0, 1, 2, 3):
-                for i in range(2):
-                    for c in range(PICKS):
-                        gather(g23[:, c, i, :], 2 + i, c, q * CH, CH)
-                src = g23[:].rearrange("p c i j -> p c j i")
-                if 2 * q + 1 in (7,):
-                    nc.vector.tensor_copy(out=packed[q][:, :, :, 2:4], in_=src)
+            for c in range(PICKS):
+                gather(g23[c][:, q * CH : (q + 1) * CH], 2, c, q * CH, CH)
+                src = g23[c][:, q * CH : (q + AHEAD + 1) * CH].rearrange("p (s j) -> p j s", j=CH)[:, :, ::AHEAD]
+                if 2 * q + c in (7,):
+                    nc.vector.tensor_copy(out=packed[q][:, c, :, 2:4], in_=src)
                 else:
-                    nc.scalar.copy(out=packed[q][:, :, :, 2:4], in_=src)
-                nc.vector.quantize_mx(out=x_codes[:].bitcast(FP8X4), scales=x_sc[:], in_=packed[q][:].rearrange("p c j i -> p (c j i)"))
+                    nc.scalar.copy(out=packed[q][:, c, :, 2:4], in_=src)
+                pick = slice(c * CH, (c + 1) * CH)
+                nc.vector.quantize_mx(out=x_codes[:, pick].bitcast(FP8X4), scales=x_sc[:, pick], in_=packed[q][:, c].rearrange("p j i -> p (j i)"))
                 for t in range(PACK):
-                    for c in range(PICKS):
-                        project(c, t, c == 0, c == PICKS - 1)
-            else:
-                for c in range(PICKS):
-                    g23 = ring.tile([P, 2, CH], F32, name="g23")
-                    for i in range(2):
-                        gather(g23[:, i, :], 2 + i, c, q * CH, CH)
-                    src = g23[:].rearrange("p i j -> p j i")
-                    if 2 * q + c in (7,):
-                        nc.vector.tensor_copy(out=packed[q][:, c, :, 2:4], in_=src)
-                    else:
-                        nc.scalar.copy(out=packed[q][:, c, :, 2:4], in_=src)
-                    pick = slice(c * CH, (c + 1) * CH)
-                    nc.vector.quantize_mx(out=x_codes[:, pick].bitcast(FP8X4), scales=x_sc[:, pick], in_=packed[q][:, c].rearrange("p j i -> p (j i)"))
-                    for t in range(PACK):
-                        project(c, t, c == 0 and t == 0, c == PICKS - 1 and t == PACK - 1)
+                    project(c, t, c == 0 and t == 0, c == PICKS - 1 and t == PACK - 1)
 
         def back(q):
             cols = slice(q * CH, (q + 1) * CH)
             y_packed = keep.tile([P, CH, PACK], BF16, name=f"y_packed{q}", align_bytes=64)
             y = keep.tile([P, PACK, CH], F32, name=f"y{q}")
-            if q in (0, 1, 2, 3):
-                nc.scalar.activation(out=y[:], in_=accs[q][:], func=ABS)
-                nc.vector.tensor_copy(out=y_packed[:], in_=y[:].rearrange("p t j -> p j t"))
-            else:
-                nc.scalar.activation(out=y_packed[:], in_=accs[q][:].rearrange("p t j -> p j t"), func=ABS)
-                nc.scalar.activation(out=y[:], in_=accs[q][:], func=ABS)
+            nc.scalar.activation(out=y[:], in_=accs[q][:], func=ABS)
+            nc.vector.tensor_copy(out=y_packed[:], in_=y[:].rearrange("p t j -> p j t"))
             nc.sync.dma_start(out=y_rows[:, :, cols], in_=y[:])
             nc.vector.quantize_mx(out=o_codes[:, cols].bitcast(FP8X4), scales=o_sc[:, cols], in_=y_packed[:].rearrange("p j t -> p (j t)"))
             if q % 2 == 1:

@@ -82,9 +82,10 @@ def tile_list_span_noneP_kernel(tc, xT, wgt, w_words, w_scales, offs, out_0, out
             nc.scalar.copy(out=packed[q][:, :, :, 0:2], in_=g01[q // 2][:, :, :, (q % 2) * CH : (q % 2 + 1) * CH].rearrange("p i c j -> p c j i"))
 
         AHEAD = 2
-        g23 = [keep.tile([P, (AHEAD + NCH) * CH], F32, name=f"g23_{c}") for c in range(PICKS)]
+        EARLY = (3, 3)
+        g23 = [keep.tile([P, (AHEAD + EARLY[c]) * CH], F32, name=f"g23_{c}") for c in range(PICKS)]
         for c in range(PICKS):
-            gather(g23[c][:, AHEAD * CH :], 3, c, 0, J)
+            gather(g23[c][:, AHEAD * CH :], 3, c, 0, EARLY[c] * CH)
 
         o_codes = keep.tile([P, J], U32, name="o_codes", align_bytes=64)
         o_sc = keep.tile([P, J], U8, name="o_sc", align_bytes=64)
@@ -109,8 +110,11 @@ def tile_list_span_noneP_kernel(tc, xT, wgt, w_words, w_scales, offs, out_0, out
                 )
 
             for c in range(PICKS):
-                gather(g23[c][:, q * CH : (q + 1) * CH], 2, c, q * CH, CH)
-                src = g23[c][:, q * CH : (q + AHEAD + 1) * CH].rearrange("p (s j) -> p j s", j=CH)[:, :, ::AHEAD]
+                s2, s3 = q % AHEAD, AHEAD + q % EARLY[c]
+                if q >= EARLY[c]:
+                    gather(g23[c][:, s3 * CH : (s3 + 1) * CH], 3, c, q * CH, CH)
+                gather(g23[c][:, s2 * CH : (s2 + 1) * CH], 2, c, q * CH, CH)
+                src = g23[c][:, s2 * CH : (s3 + 1) * CH].rearrange("p (s j) -> p j s", j=CH)[:, :, :: s3 - s2]
                 if 2 * q + c in (7,):
                     nc.vector.tensor_copy(out=packed[q][:, c, :, 2:4], in_=src)
                 else:

@@ -1,6 +1,7 @@
 from contextlib import ExitStack
 
 import concourse.mybir as mybir
+from concourse.masks import make_identity
 
 K, N, T, J = 512, 512, 2048, 512
 FLOPS = 2 * 2 * K * N * J
@@ -31,46 +32,73 @@ def tile_list_span_noneP_kernel(tc, xT, wgt, w_words, w_scales, offs, out_0, out
         keep = ctx.enter_context(tc.tile_pool(name="keep", bufs=1))
         psum = ctx.enter_context(tc.psum_pool(name="psum", bufs=1))
 
+        HALF = J // 2
         ws_raw = keep.tile([P, N], U8, name="ws_raw", align_bytes=64)
         nc.gpsimd.memset(ws_raw[:].bitcast(I32), 0)
+        ident = keep.tile([P, P], F32, name="ident")
+        make_identity(nc, ident[:])
         offsets = keep.tile([P, PICKS * J // LIST_ROWS], U16, name="offsets")
-        nc.sync.dma_start(offsets[:], offs)
 
         w_raw = keep.tile([P, 2 * N], U8, name="w_raw", align_bytes=64)
         x_rows = xT.rearrange("(p i) t -> p i t", i=PACK)
-        wg = [keep.tile([P, J], F32, name=f"wg{c}") for c in range(PICKS)]
+        first = keep.tile([P, PICKS, J], F32, name="first")
+        signed = [first[:, c, :] for c in range(PICKS)]
         xs = [keep.tile([P, T], F32, name=f"x{i}") for i in range(PACK)]
+        few = keep.tile([P, P], F32, name="few")
+        nc.sync.dma_start(out=few[0:64, :], in_=wgt[:, J + HALF :].rearrange("(q e) (c u) -> q e c u", e=4, u=P)[:, 0])
+        nc.sync.dma_start(out=few[64:128, :], in_=wgt[:, 0:J].rearrange("(q e) (c u) -> q e c u", e=8, u=P)[:, 0])
         nc.sync.dma_start(out=w_raw[:].bitcast(I32), in_=w_words[0].bitcast(I32))
-        nc.sync.dma_start(out=wg[0][:], in_=wgt[:, 0:J])
-        for q in range(4):
-            nc.sync.dma_start(out=ws_raw[32 * q : 32 * q + 4, :].bitcast(I32), in_=w_scales[0, 4 * q : 4 * q + 4, :].bitcast(I32))
+        nc.sync.dma_start(out=signed[1][:, 0:HALF], in_=wgt[:, J : J + HALF])
+        nc.sync.dma_start(out=ws_raw[0:16, :].bitcast(I32), in_=w_scales[0].bitcast(I32))
         nc.sync.dma_start(out=xs[0][:], in_=x_rows[:, 0, :])
-        nc.sync.dma_start(out=wg[1][:], in_=wgt[:, J : 2 * J])
+        nc.sync.dma_start(offsets[:], offs)
         for i in (1, 3, 2):
             nc.sync.dma_start(out=xs[i][:], in_=x_rows[:, i, :])
+
+        turned = psum.tile([P, P], F32, name="turned")
+        nc.tensor.transpose(turned[:], few[:], ident[:])
+        by_block = [
+            turned[:, 0:64].rearrange("u (q c) -> u c q", c=2),
+            turned[:, 64:128].rearrange("u (q c) -> u c q", c=4)[:, 0:2, :],
+            turned[:, 64:128].rearrange("u (q c) -> u c q", c=4)[:, 2:4, :],
+        ]
+        places = [signed[1][:, HALF:], signed[0][:, 0:HALF], signed[0][:, HALF:]]
+        for k in range(3):
+            rows = by_block[k].shape[2]
+            wide = keep.tile([P, 2, P], F32, name=f"wide{k}")
+            nc.scalar.activation(
+                out=wide[:].rearrange("u c (q r) -> u c q r", q=rows),
+                in_=by_block[k].unsqueeze(3).to_broadcast([P, 2, rows, P // rows]),
+                func=COPY,
+                scale=1.0 if k == 0 else -1.0,
+            )
+            back_again = psum.tile([P, 2, P], F32, name=f"spread{k}")
+            for c in range(2):
+                nc.tensor.transpose(back_again[:, c, :], wide[:, c, :], ident[:])
+            nc.scalar.copy(out=places[k], in_=back_again[:].rearrange("p c u -> p (c u)"))
+
+        later = keep.tile([P, PICKS, J], F32, name="later")
+        nc.scalar.copy(out=later[:], in_=first[:])
 
         w_codes = keep.tile([P, 2 * N], U8, name="w_codes", align_bytes=64)
         w_sc = keep.tile([P, N], U8, name="w_sc", align_bytes=64)
         nc.vector.tensor_copy(
-            out=w_codes[:].rearrange("p (t m b) -> p t m b", t=PACK, b=2),
-            in_=w_raw[:].rearrange("p (m t b) -> p t m b", t=PACK, b=2),
+            out=w_codes[:].bitcast(U16).rearrange("p (t m) -> p t m", t=PACK),
+            in_=w_raw[:].bitcast(U16).rearrange("p (m t) -> p t m", t=PACK),
         )
         nc.vector.tensor_copy(
             out=w_sc[:].rearrange("p (t m) -> p t m", t=PACK),
             in_=ws_raw[:].rearrange("p (m t) -> p t m", t=PACK),
         )
-
-        wneg = keep.tile([P, J], F32, name="wneg")
-        nc.scalar.activation(out=wneg[:], in_=wg[0][:], func=COPY, scale=-1.0)
-        signed = [wneg, wg[1]]
+        for q in range(1, 4):
+            nc.sync.dma_start(out=w_sc[32 * q : 32 * q + 4, :].bitcast(I32), in_=w_sc[4 * q : 4 * q + 4, :].bitcast(I32))
 
         def gather(dst, i, c, j0, width):
             a = (c * J + j0) // LIST_ROWS
-            nc.vector.tensor_tensor(dst, xs[i][:].indirect(offsets[:, a : a + width // LIST_ROWS]), signed[c][:, j0 : j0 + width], MULT)
+            nc.vector.tensor_tensor(dst, xs[i][:].indirect(offsets[:, a : a + width // LIST_ROWS]), (first if i == 0 else later)[:, c, j0 : j0 + width], MULT)
 
-        HALF = J // 2
         g01 = [keep.tile([P, 2, PICKS, HALF], F32, name=f"g01_{h}") for h in range(2)]
-        for c in range(PICKS):
+        for c in (1, 0):
             for h in range(2):
                 gather(g01[h][:, 0, c, :], 0, c, h * HALF, HALF)
         for h in range(2):

@@ -41,44 +41,35 @@ def tile_list_span_noneP_kernel(tc, xT, wgt, w_words, w_scales, offs, out_0, out
 
         w_raw = keep.tile([P, 2 * N], U8, name="w_raw", align_bytes=64)
         x_rows = xT.rearrange("(p i) t -> p i t", i=PACK)
-        first = keep.tile([P, PICKS, J], F32, name="first")
-        signed = [first[:, c, :] for c in range(PICKS)]
+        signed = [keep.tile([P, J], F32, name=f"signed{c}") for c in range(PICKS)]
         xs = [keep.tile([P, T], F32, name=f"x{i}") for i in range(PACK)]
         few = keep.tile([P, P], F32, name="few")
-        nc.sync.dma_start(out=few[0:64, :], in_=wgt[:, J + HALF :].rearrange("(q e) (c u) -> q e c u", e=4, u=P)[:, 0])
-        nc.sync.dma_start(out=few[64:128, :], in_=wgt[:, 0:J].rearrange("(q e) (c u) -> q e c u", e=8, u=P)[:, 0])
+        opening = keep.tile([P, HALF], F32, name="opening")
+        nc.sync.dma_start(out=few[:], in_=wgt.rearrange("(q e) (b u) -> q e b u", e=8, u=P)[:, 0])
         nc.sync.dma_start(out=w_raw[:].bitcast(I32), in_=w_words[0].bitcast(I32))
-        nc.sync.dma_start(out=signed[1][:, 0:HALF], in_=wgt[:, J : J + HALF])
-        nc.sync.dma_start(out=ws_raw[0:16, :].bitcast(I32), in_=w_scales[0].bitcast(I32))
+        nc.sync.dma_start(out=opening[:], in_=wgt[:, J : J + HALF])
+        for q in range(4):
+            nc.sync.dma_start(out=ws_raw[32 * q : 32 * q + 4, :].bitcast(I32), in_=w_scales[0, 4 * q : 4 * q + 4, :].bitcast(I32))
         nc.sync.dma_start(out=xs[0][:], in_=x_rows[:, 0, :])
         nc.sync.dma_start(offsets[:], offs)
         for i in (1, 3, 2):
             nc.sync.dma_start(out=xs[i][:], in_=x_rows[:, i, :])
 
-        turned = psum.tile([P, P], F32, name="turned")
+        turned = psum.tile([P, P], F32, name="turned", tag="acc3")
         nc.tensor.transpose(turned[:], few[:], ident[:])
-        by_block = [
-            turned[:, 0:64].rearrange("u (q c) -> u c q", c=2),
-            turned[:, 64:128].rearrange("u (q c) -> u c q", c=4)[:, 0:2, :],
-            turned[:, 64:128].rearrange("u (q c) -> u c q", c=4)[:, 2:4, :],
-        ]
-        places = [signed[1][:, HALF:], signed[0][:, 0:HALF], signed[0][:, HALF:]]
-        for k in range(3):
-            rows = by_block[k].shape[2]
-            wide = keep.tile([P, 2, P], F32, name=f"wide{k}")
+        blocks = turned[:].rearrange("u (q b) -> u b q", b=8)
+        for c, h in ((1, 1), (0, 1), (0, 0), (1, 0)):
+            wide = keep.tile([P, 2, P], F32, name=f"wide{c}{h}")
             nc.scalar.activation(
-                out=wide[:].rearrange("u c (q r) -> u c q r", q=rows),
-                in_=by_block[k].unsqueeze(3).to_broadcast([P, 2, rows, P // rows]),
+                out=wide[:].rearrange("u b (q r) -> u b q r", r=8),
+                in_=blocks[:, 4 * c + 2 * h : 4 * c + 2 * h + 2, :].unsqueeze(3).to_broadcast([P, 2, 16, 8]),
                 func=COPY,
-                scale=1.0 if k == 0 else -1.0,
+                scale=1.0 if c == 1 else -1.0,
             )
-            back_again = psum.tile([P, 2, P], F32, name=f"spread{k}")
-            for c in range(2):
-                nc.tensor.transpose(back_again[:, c, :], wide[:, c, :], ident[:])
-            nc.scalar.copy(out=places[k], in_=back_again[:].rearrange("p c u -> p (c u)"))
-
-        later = keep.tile([P, PICKS, J], F32, name="later")
-        nc.scalar.copy(out=later[:], in_=first[:])
+            spread = psum.tile([P, 2, P], F32, name=f"spread{c}{h}")
+            for b in range(2):
+                nc.tensor.transpose(spread[:, b, :], wide[:, b, :], ident[:])
+            nc.scalar.copy(out=signed[c][:, h * HALF : (h + 1) * HALF], in_=spread[:].rearrange("p b u -> p (b u)"))
 
         w_codes = keep.tile([P, 2 * N], U8, name="w_codes", align_bytes=64)
         w_sc = keep.tile([P, N], U8, name="w_sc", align_bytes=64)
@@ -90,24 +81,25 @@ def tile_list_span_noneP_kernel(tc, xT, wgt, w_words, w_scales, offs, out_0, out
             out=w_sc[:].rearrange("p (t m) -> p t m", t=PACK),
             in_=ws_raw[:].rearrange("p (m t) -> p t m", t=PACK),
         )
-        for q in range(1, 4):
-            nc.sync.dma_start(out=w_sc[32 * q : 32 * q + 4, :].bitcast(I32), in_=w_sc[4 * q : 4 * q + 4, :].bitcast(I32))
 
-        def gather(dst, i, c, j0, width):
+        def gather(dst, i, c, j0, width, weights=None):
             a = (c * J + j0) // LIST_ROWS
-            nc.vector.tensor_tensor(dst, xs[i][:].indirect(offsets[:, a : a + width // LIST_ROWS]), (first if i == 0 else later)[:, c, j0 : j0 + width], MULT)
+            if weights is None:
+                weights = signed[c][:, j0 : j0 + width]
+            nc.vector.tensor_tensor(dst, xs[i][:].indirect(offsets[:, a : a + width // LIST_ROWS]), weights, MULT)
 
-        g01 = [keep.tile([P, 2, PICKS, HALF], F32, name=f"g01_{h}") for h in range(2)]
-        for c in (1, 0):
+        g01 = [keep.tile([P, 2, J], F32, name=f"g01_{c}") for c in range(PICKS)]
+        gather(g01[1][:, 0, 0:HALF], 0, 1, 0, HALF, opening[:])
+        for c, h in ((1, 1), (0, 1), (0, 0)):
+            gather(g01[c][:, 0, h * HALF : (h + 1) * HALF], 0, c, h * HALF, HALF)
+        for c in range(PICKS):
+            gather(g01[c][:, 1, :], 1, c, 0, J)
+
+        halves = [keep.tile([P, PICKS, HALF, PACK], BF16, name=f"packed{h}", align_bytes=64) for h in range(2)]
+        packed = [halves[q // 2][:, :, (q % 2) * CH : (q % 2 + 1) * CH, :] for q in range(NCH)]
+        for c in range(PICKS):
             for h in range(2):
-                gather(g01[h][:, 0, c, :], 0, c, h * HALF, HALF)
-        for h in range(2):
-            for c in range(PICKS):
-                gather(g01[h][:, 1, c, :], 1, c, h * HALF, HALF)
-
-        packed = [keep.tile([P, PICKS, CH, PACK], BF16, name=f"packed{q}", align_bytes=64) for q in range(NCH)]
-        for q in range(NCH):
-            nc.scalar.copy(out=packed[q][:, :, :, 0:2], in_=g01[q // 2][:, :, :, (q % 2) * CH : (q % 2 + 1) * CH].rearrange("p i c j -> p c j i"))
+                nc.scalar.copy(out=halves[h][:, c, :, 0:2], in_=g01[c][:, :, h * HALF : (h + 1) * HALF].rearrange("p i j -> p j i"))
 
         AHEAD = 2
         EARLY = (3, 3)
@@ -120,7 +112,7 @@ def tile_list_span_noneP_kernel(tc, xT, wgt, w_words, w_scales, offs, out_0, out
         y_rows = out_0.rearrange("(p t) j -> p t j", t=PACK)
         o_words = out_1[0].rearrange("p j i -> p (j i)").bitcast(I32)
 
-        accs = [psum.tile([P, PACK, CH], F32, name=f"acc{q}") for q in range(NCH)]
+        accs = [psum.tile([P, PACK, CH], F32, name=f"acc{q}", tag=f"acc{q}") for q in range(NCH)]
 
         def front(q):
             x_codes = keep.tile([P, PICKS * CH], U32, name=f"x_codes{q}", align_bytes=64)

@@ -44,12 +44,11 @@ def tile_list_span_noneP_kernel(tc, xT, wgt, w_words, w_scales, offs, out_0, out
         signed = [keep.tile([P, J], F32, name=f"signed{c}") for c in range(PICKS)]
         xs = [keep.tile([P, T], F32, name=f"x{i}") for i in range(PACK)]
         few = keep.tile([P, P], F32, name="few")
-        opening = keep.tile([P, HALF], F32, name="opening")
+        opening = keep.tile([P, CH], F32, name="opening")
         nc.sync.dma_start(out=few[:], in_=wgt.rearrange("(q e) (b u) -> q e b u", e=8, u=P)[:, 0])
         nc.sync.dma_start(out=w_raw[:].bitcast(I32), in_=w_words[0].bitcast(I32))
-        nc.sync.dma_start(out=opening[:], in_=wgt[:, J : J + HALF])
-        for q in range(4):
-            nc.sync.dma_start(out=ws_raw[32 * q : 32 * q + 4, :].bitcast(I32), in_=w_scales[0, 4 * q : 4 * q + 4, :].bitcast(I32))
+        nc.sync.dma_start(out=opening[:], in_=wgt[:, J : J + CH])
+        nc.sync.dma_start(out=ws_raw[0:16, :].bitcast(I32), in_=w_scales[0].bitcast(I32))
         nc.sync.dma_start(out=xs[0][:], in_=x_rows[:, 0, :])
         nc.sync.dma_start(offsets[:], offs)
         for i in (1, 3, 2):
@@ -81,6 +80,8 @@ def tile_list_span_noneP_kernel(tc, xT, wgt, w_words, w_scales, offs, out_0, out
             out=w_sc[:].rearrange("p (t m) -> p t m", t=PACK),
             in_=ws_raw[:].rearrange("p (m t) -> p t m", t=PACK),
         )
+        for q in range(1, 4):
+            nc.gpsimd.dma_start(out=w_sc[32 * q : 32 * q + 4, :].bitcast(I32), in_=w_sc[4 * q : 4 * q + 4, :].bitcast(I32))
 
         def gather(dst, i, c, j0, width, weights=None):
             a = (c * J + j0) // LIST_ROWS
@@ -89,9 +90,10 @@ def tile_list_span_noneP_kernel(tc, xT, wgt, w_words, w_scales, offs, out_0, out
             nc.vector.tensor_tensor(dst, xs[i][:].indirect(offsets[:, a : a + width // LIST_ROWS]), weights, MULT)
 
         g01 = [keep.tile([P, 2, J], F32, name=f"g01_{c}") for c in range(PICKS)]
-        gather(g01[1][:, 0, 0:HALF], 0, 1, 0, HALF, opening[:])
+        gather(g01[1][:, 0, 0:CH], 0, 1, 0, CH, opening[:])
         for c, h in ((1, 1), (0, 1), (0, 0)):
             gather(g01[c][:, 0, h * HALF : (h + 1) * HALF], 0, c, h * HALF, HALF)
+        gather(g01[1][:, 0, CH:HALF], 0, 1, CH, CH)
         for c in range(PICKS):
             gather(g01[c][:, 1, :], 1, c, 0, J)
 

@@ -65,7 +65,7 @@ def tile_list_span_noneP_kernel(tc, xT, wgt, w_words, w_scales, offs, out_0, out
                 func=COPY,
                 scale=1.0 if c == 1 else -1.0,
             )
-            spread = psum.tile([P, 2, P], F32, name=f"spread{c}{h}")
+            spread = psum.tile([P, 2, P], F32, name=f"spread{c}{h}", tag=f"spread{c}{h}")
             for b in range(2):
                 nc.tensor.transpose(spread[:, b, :], wide[:, b, :], ident[:])
             nc.scalar.copy(out=signed[c][:, h * HALF : (h + 1) * HALF], in_=spread[:].rearrange("p b u -> p (b u)"))
@@ -115,6 +115,10 @@ def tile_list_span_noneP_kernel(tc, xT, wgt, w_words, w_scales, offs, out_0, out
         o_words = out_1[0].rearrange("p j i -> p (j i)").bitcast(I32)
 
         accs = [psum.tile([P, PACK, CH], F32, name=f"acc{q}", tag=f"acc{q}") for q in range(NCH)]
+        last_b = psum.tile([P, 2, CH], F32, name="last_b", tag="spread11")
+
+        def place(q, t):
+            return last_b[:, t - 2, :] if q == NCH - 1 and t >= 2 else accs[q][:, t, :]
 
         def front(q):
             x_codes = keep.tile([P, PICKS * CH], U32, name=f"x_codes{q}", align_bytes=64)
@@ -122,7 +126,7 @@ def tile_list_span_noneP_kernel(tc, xT, wgt, w_words, w_scales, offs, out_0, out
 
             def project(c, t, start, stop):
                 nc.tensor.matmul_mx(
-                    out=accs[q][:, t, :],
+                    out=place(q, t),
                     lhsT=w_codes[:, 2 * P * t : 2 * P * (t + 1)].bitcast(FP4X4),
                     lhsT_scale=w_sc[:, P * t : P * (t + 1)],
                     rhs=x_codes[:, c * CH : (c + 1) * CH].bitcast(FP8X4),
@@ -144,16 +148,30 @@ def tile_list_span_noneP_kernel(tc, xT, wgt, w_words, w_scales, offs, out_0, out
                 pick = slice(c * CH, (c + 1) * CH)
                 nc.vector.quantize_mx(out=x_codes[:, pick].bitcast(FP8X4), scales=x_sc[:, pick], in_=packed[q][:, c].rearrange("p j i -> p (j i)"))
                 for t in range(PACK):
-                    project(c, t, c == 0 and t == 0, c == PICKS - 1 and t == PACK - 1)
+                    width = 2 if q == NCH - 1 else PACK
+                    project(c, t, c == 0 and t % width == 0, c == PICKS - 1 and t % width == width - 1)
+
+        y_pairs = [keep.tile([P, 2 * CH, PACK], BF16, name=f"y_packed{h}", align_bytes=64) for h in range(2)]
 
         def back(q):
             cols = slice(q * CH, (q + 1) * CH)
-            y_packed = keep.tile([P, CH, PACK], BF16, name=f"y_packed{q}", align_bytes=64)
-            y = keep.tile([P, PACK, CH], F32, name=f"y{q}")
-            nc.scalar.activation(out=y[:], in_=accs[q][:], func=ABS)
-            nc.vector.tensor_copy(out=y_packed[:], in_=y[:].rearrange("p t j -> p j t"))
-            nc.sync.dma_start(out=y_rows[:, :, cols], in_=y[:])
-            nc.vector.quantize_mx(out=o_codes[:, cols].bitcast(FP8X4), scales=o_sc[:, cols], in_=y_packed[:].rearrange("p j t -> p (j t)"))
+            y_packed = y_pairs[q // 2][:, (q % 2) * CH : (q % 2 + 1) * CH, :]
+            if q == NCH - 1:
+                y = keep.tile([P, PACK, CH], F32, name=f"y{q}")
+                for u, bank in enumerate((accs[q][:, 0:2, :], last_b[:])):
+                    nc.scalar.activation(out=y[:, 2 * u : 2 * u + 2, :], in_=bank, func=ABS)
+                    nc.vector.tensor_copy(out=y_packed[:, :, 2 * u : 2 * u + 2], in_=y[:, 2 * u : 2 * u + 2, :].rearrange("p t j -> p j t"))
+                nc.sync.dma_start(out=y_rows[:, :, cols], in_=y[:])
+            else:
+                y = keep.tile([P, PACK, CH], F32, name=f"y{q}")
+                nc.scalar.activation(out=y[:], in_=accs[q][:], func=ABS)
+                nc.vector.tensor_copy(out=y_packed, in_=y[:].rearrange("p t j -> p j t"))
+                nc.sync.dma_start(out=y_rows[:, :, cols], in_=y[:])
+            if q == 1:
+                done = slice(0, 2 * CH)
+                nc.vector.quantize_mx(out=o_codes[:, done].bitcast(FP8X4), scales=o_sc[:, done], in_=y_pairs[0][:].rearrange("p j t -> p (j t)"))
+            if q >= 2:
+                nc.vector.quantize_mx(out=o_codes[:, cols].bitcast(FP8X4), scales=o_sc[:, cols], in_=y_packed.rearrange("p j t -> p (j t)"))
             if q % 2 == 1:
                 done = slice((q - 1) * CH, (q + 1) * CH)
                 nc.sync.dma_start(out=o_words[:, done], in_=o_codes[:, done].bitcast(I32))
@@ -165,5 +183,4 @@ def tile_list_span_noneP_kernel(tc, xT, wgt, w_words, w_scales, offs, out_0, out
             if q >= LAG:
                 back(q - LAG)
         for q in range(4):
-            eng = nc.sync if q < 2 else nc.scalar
-            eng.dma_start(out=out_2[0, 4 * q : 4 * q + 4, :].bitcast(I32), in_=o_sc[32 * q : 32 * q + 4, :].bitcast(I32))
+            nc.sync.dma_start(out=out_2[0, 4 * q : 4 * q + 4, :].bitcast(I32), in_=o_sc[32 * q : 32 * q + 4, :].bitcast(I32))

@@ -41,13 +41,12 @@ def tile_list_span_noneP_kernel(tc, xT, wgt, w_words, w_scales, offs, out_0, out
 
         w_raw = keep.tile([P, 2 * N], U8, name="w_raw", align_bytes=64)
         x_rows = xT.rearrange("(p i) t -> p i t", i=PACK)
-        signed = [keep.tile([P, J], F32, name=f"signed{c}") for c in range(PICKS)]
-        xs = [keep.tile([P, T], F32, name=f"x{i}") for i in range(PACK)]
+        signed = keep.tile([P, PICKS * J], F32, name="signed")
+        xs = [keep.tile([P, T], F32, name=f"x{i}", tag=f"x{i}") for i in range(PACK)]
         few = keep.tile([P, P], F32, name="few")
-        opening = keep.tile([P, CH], F32, name="opening")
-        nc.sync.dma_start(out=few[:], in_=wgt.rearrange("(q e) (b u) -> q e b u", e=8, u=P)[:, 0])
+        nc.gpsimd.memset(few[P // 2 :, :], 0.0)
+        nc.sync.dma_start(out=few[: P // 2, :], in_=wgt.rearrange("(q e) (b u) -> q e b u", e=16, u=P)[:, 0])
         nc.sync.dma_start(out=w_raw[:].bitcast(I32), in_=w_words[0].bitcast(I32))
-        nc.sync.dma_start(out=opening[:], in_=wgt[:, J : J + CH])
         nc.sync.dma_start(out=ws_raw[0:16, :].bitcast(I32), in_=w_scales[0].bitcast(I32))
         nc.sync.dma_start(out=xs[0][:], in_=x_rows[:, 0, :])
         nc.sync.dma_start(offsets[:], offs)
@@ -56,19 +55,25 @@ def tile_list_span_noneP_kernel(tc, xT, wgt, w_words, w_scales, offs, out_0, out
 
         turned = psum.tile([P, P], F32, name="turned", tag="acc3")
         nc.tensor.transpose(turned[:], few[:], ident[:])
-        blocks = turned[:].rearrange("u (q b) -> u b q", b=8)
-        for c, h in ((1, 1), (0, 1), (0, 0), (1, 0)):
-            wide = keep.tile([P, 2, P], F32, name=f"wide{c}{h}")
-            nc.scalar.activation(
-                out=wide[:].rearrange("u b (q r) -> u b q r", r=8),
-                in_=blocks[:, 4 * c + 2 * h : 4 * c + 2 * h + 2, :].unsqueeze(3).to_broadcast([P, 2, 16, 8]),
-                func=COPY,
-                scale=1.0 if c == 1 else -1.0,
-            )
-            spread = psum.tile([P, 2, P], F32, name=f"spread{c}{h}", tag=f"spread{c}{h}")
-            for b in range(2):
-                nc.tensor.transpose(spread[:, b, :], wide[:, b, :], ident[:])
-            nc.scalar.copy(out=signed[c][:, h * HALF : (h + 1) * HALF], in_=spread[:].rearrange("p b u -> p (b u)"))
+        blocks = turned[:, : P // 2].rearrange("u (q b) -> u b q", b=8)
+        runs = ((3,), (0,), (1, 2))
+        for n, quarters in enumerate(runs):
+            spread = psum.tile([P, 2 * len(quarters), P], F32, name=f"spread{n}", tag=f"spread{n}")
+            for m, v in enumerate(quarters):
+                wide = keep.tile([P, 2, P], F32, name=f"wide{v}")
+                nc.scalar.activation(
+                    out=wide[:].rearrange("u b (q r) -> u b q r", r=16),
+                    in_=blocks[:, 2 * v : 2 * v + 2, :].unsqueeze(3).to_broadcast([P, 2, 8, 16]),
+                    func=COPY,
+                    scale=1.0 if v >= 2 else -1.0,
+                )
+                for b in range(2):
+                    nc.tensor.transpose(spread[:, 2 * m + b, :], wide[:, b, :], ident[:])
+            cols = slice(quarters[0] * HALF, (quarters[-1] + 1) * HALF)
+            if n == 0:
+                nc.vector.tensor_copy(out=signed[:, cols], in_=spread[:].rearrange("p b u -> p (b u)"))
+            else:
+                nc.scalar.copy(out=signed[:, cols], in_=spread[:].rearrange("p b u -> p (b u)"))
 
         w_codes = keep.tile([P, 2 * N], U8, name="w_codes", align_bytes=64)
         w_sc = keep.tile([P, N], U8, name="w_sc", align_bytes=64)
@@ -83,29 +88,28 @@ def tile_list_span_noneP_kernel(tc, xT, wgt, w_words, w_scales, offs, out_0, out
         for q in range(1, 4):
             nc.gpsimd.dma_start(out=w_sc[32 * q : 32 * q + 4, :].bitcast(I32), in_=w_sc[4 * q : 4 * q + 4, :].bitcast(I32))
 
-        def gather(dst, i, c, j0, width, weights=None):
-            a = (c * J + j0) // LIST_ROWS
-            if weights is None:
-                weights = signed[c][:, j0 : j0 + width]
-            nc.vector.tensor_tensor(dst, xs[i][:].indirect(offsets[:, a : a + width // LIST_ROWS]), weights, MULT)
+        def gather(dst, i, c, j0, width):
+            a = c * J + j0
+            nc.vector.tensor_tensor(dst, xs[i][:].indirect(offsets[:, a // LIST_ROWS : (a + width) // LIST_ROWS]), signed[:, a : a + width], MULT)
 
-        g01 = [keep.tile([P, 2, J], F32, name=f"g01_{c}") for c in range(PICKS)]
-        gather(g01[1][:, 0, 0:CH], 0, 1, 0, CH, opening[:])
-        for c, h in ((1, 1), (0, 1), (0, 0)):
-            gather(g01[c][:, 0, h * HALF : (h + 1) * HALF], 0, c, h * HALF, HALF)
-        gather(g01[1][:, 0, CH:HALF], 0, 1, CH, CH)
+        g01 = keep.tile([P, 2, PICKS * J], F32, name="g01")
+        for quarters in runs:
+            a, width = quarters[0] * HALF, len(quarters) * HALF
+            gather(g01[:, 0, a : a + width], 0, 0, a, width)
         for c in range(PICKS):
-            gather(g01[c][:, 1, :], 1, c, 0, J)
+            gather(g01[:, 1, c * J : (c + 1) * J], 1, c, 0, J)
 
         halves = [keep.tile([P, PICKS, HALF, PACK], BF16, name=f"packed{h}", align_bytes=64) for h in range(2)]
         packed = [halves[q // 2][:, :, (q % 2) * CH : (q % 2 + 1) * CH, :] for q in range(NCH)]
         for c in range(PICKS):
             for h in range(2):
-                nc.scalar.copy(out=halves[h][:, c, :, 0:2], in_=g01[c][:, :, h * HALF : (h + 1) * HALF].rearrange("p i j -> p j i"))
+                nc.scalar.copy(out=halves[h][:, c, :, 0:2], in_=g01[:, :, c * J + h * HALF : c * J + (h + 1) * HALF].rearrange("p i j -> p j i"))
 
         AHEAD = 2
         EARLY = (3, 3)
-        g23 = [keep.tile([P, (AHEAD + EARLY[c]) * CH], F32, name=f"g23_{c}") for c in range(PICKS)]
+        SLOTS = AHEAD + max(EARLY)
+        slots = keep.tile([P, PICKS * SLOTS * CH], F32, name="slots", tag="x0")
+        g23 = [slots[:, c * SLOTS * CH : (c + 1) * SLOTS * CH] for c in range(PICKS)]
         for c in range(PICKS):
             gather(g23[c][:, AHEAD * CH :], 3, c, 0, EARLY[c] * CH)
 
@@ -115,7 +119,7 @@ def tile_list_span_noneP_kernel(tc, xT, wgt, w_words, w_scales, offs, out_0, out
         o_words = out_1[0].rearrange("p j i -> p (j i)").bitcast(I32)
 
         accs = [psum.tile([P, PACK, CH], F32, name=f"acc{q}", tag=f"acc{q}") for q in range(NCH)]
-        last_b = psum.tile([P, 2, CH], F32, name="last_b", tag="spread11")
+        last_b = psum.tile([P, 2, CH], F32, name="last_b", tag="spread0")
 
         def place(q, t):
             return last_b[:, t - 2, :] if q == NCH - 1 and t >= 2 else accs[q][:, t, :]

@@ -33,7 +33,7 @@ def tile_list_span_noneP_kernel(tc, xT, wgt, w_words, w_scales, offs, out_0, out
         psum = ctx.enter_context(tc.psum_pool(name="psum", bufs=1))
 
         HALF = J // 2
-        ws_raw = keep.tile([P, N], U8, name="ws_raw", align_bytes=64)
+        ws_raw = keep.tile([P, N], U8, name="ws_raw", tag="ws_raw", align_bytes=64)
         nc.gpsimd.memset(ws_raw[:].bitcast(I32), 0)
         ident = keep.tile([P, P], F32, name="ident")
         make_identity(nc, ident[:])
@@ -42,7 +42,7 @@ def tile_list_span_noneP_kernel(tc, xT, wgt, w_words, w_scales, offs, out_0, out
         w_raw = keep.tile([P, 2 * N], U8, name="w_raw", align_bytes=64)
         x_rows = xT.rearrange("(p i) t -> p i t", i=PACK)
         signed = keep.tile([P, PICKS * J], F32, name="signed")
-        xs = [keep.tile([P, T], F32, name=f"x{i}", tag=f"x{i}") for i in range(PACK)]
+        xs = {i: keep.tile([P, T], F32, name=f"x{i}", tag=f"x{i}") for i in (0, 1)}
         few = keep.tile([P, P], F32, name="few")
         nc.gpsimd.memset(few[P // 2 :, :], 0.0)
         nc.sync.dma_start(out=few[: P // 2, :], in_=wgt.rearrange("(q e) (b u) -> q e b u", e=16, u=P)[:, 0])
@@ -50,8 +50,7 @@ def tile_list_span_noneP_kernel(tc, xT, wgt, w_words, w_scales, offs, out_0, out
         nc.sync.dma_start(out=ws_raw[0:16, :].bitcast(I32), in_=w_scales[0].bitcast(I32))
         nc.sync.dma_start(out=xs[0][:], in_=x_rows[:, 0, :])
         nc.sync.dma_start(offsets[:], offs)
-        for i in (1, 3, 2):
-            nc.sync.dma_start(out=xs[i][:], in_=x_rows[:, i, :])
+        nc.sync.dma_start(out=xs[1][:], in_=x_rows[:, 1, :])
 
         turned = psum.tile([P, P], F32, name="turned", tag="acc3")
         nc.tensor.transpose(turned[:], few[:], ident[:])
@@ -60,7 +59,7 @@ def tile_list_span_noneP_kernel(tc, xT, wgt, w_words, w_scales, offs, out_0, out
         for n, quarters in enumerate(runs):
             spread = psum.tile([P, 2 * len(quarters), P], F32, name=f"spread{n}", tag=f"spread{n}")
             for m, v in enumerate(quarters):
-                wide = keep.tile([P, 2, P], F32, name=f"wide{v}")
+                wide = keep.tile([P, 2, P], F32, name=f"wide{v}", tag=f"wide{v}")
                 nc.scalar.activation(
                     out=wide[:].rearrange("u b (q r) -> u b q r", r=16),
                     in_=blocks[:, 2 * v : 2 * v + 2, :].unsqueeze(3).to_broadcast([P, 2, 8, 16]),
@@ -86,7 +85,11 @@ def tile_list_span_noneP_kernel(tc, xT, wgt, w_words, w_scales, offs, out_0, out
             in_=ws_raw[:].rearrange("p (m t) -> p t m", t=PACK),
         )
         for q in range(1, 4):
-            nc.gpsimd.dma_start(out=w_sc[32 * q : 32 * q + 4, :].bitcast(I32), in_=w_sc[4 * q : 4 * q + 4, :].bitcast(I32))
+            nc.sync.dma_start(out=w_sc[32 * q : 32 * q + 4, :].bitcast(I32), in_=w_sc[4 * q : 4 * q + 4, :].bitcast(I32))
+        xs[3] = keep.tile([P, T], F32, name="x3", tag="ws_raw", align_bytes=64)
+        xs[2] = keep.tile([P, T], F32, name="x2", tag="wide2")
+        for i in (3, 2):
+            nc.sync.dma_start(out=xs[i][:], in_=x_rows[:, i, :])
 
         def gather(dst, i, c, j0, width):
             a = c * J + j0

@@ -42,7 +42,7 @@ def tile_list_span_noneP_kernel(tc, xT, wgt, w_words, w_scales, offs, out_0, out
         w_raw = keep.tile([P, 2 * N], U8, name="w_raw", align_bytes=64)
         x_rows = xT.rearrange("(p i) t -> p i t", i=PACK)
         signed = keep.tile([P, PICKS * J], F32, name="signed")
-        xs = {i: keep.tile([P, T], F32, name=f"x{i}", tag=f"x{i}") for i in (0, 1)}
+        xs = {i: keep.tile([P, T], F32, name=f"x{i}", tag=f"x{i}", align_bytes=64) for i in (0, 1)}
         few = keep.tile([P, P], F32, name="few")
         nc.gpsimd.memset(few[P // 2 :, :], 0.0)
         nc.sync.dma_start(out=few[: P // 2, :], in_=wgt.rearrange("(q e) (b u) -> q e b u", e=16, u=P)[:, 0])
@@ -108,13 +108,24 @@ def tile_list_span_noneP_kernel(tc, xT, wgt, w_words, w_scales, offs, out_0, out
             for h in range(2):
                 nc.scalar.copy(out=halves[h][:, c, :, 0:2], in_=g01[:, :, c * J + h * HALF : c * J + (h + 1) * HALF].rearrange("p i j -> p j i"))
 
-        AHEAD = 2
-        EARLY = (3, 3)
-        SLOTS = AHEAD + max(EARLY)
-        slots = keep.tile([P, PICKS * SLOTS * CH], F32, name="slots", tag="x0")
-        g23 = [slots[:, c * SLOTS * CH : (c + 1) * SLOTS * CH] for c in range(PICKS)]
+        PIECES = PICKS * NCH
+        RING = 4
+        EARLY = 3
+        slots = keep.tile([P, (RING + PICKS * EARLY) * CH], F32, name="slots", tag="x0", align_bytes=64)
+
+        def slot(s, count=1):
+            return slots[:, s * CH : (s + count) * CH]
+
+        def slots_of(piece):
+            q, c = divmod(piece, PICKS)
+            if piece == PIECES - 1:
+                return 1, RING + c * EARLY + 1
+            if q >= EARLY:
+                return piece % RING, RING + c * EARLY + 1
+            return piece % RING, RING + c * EARLY + q
+
         for c in range(PICKS):
-            gather(g23[c][:, AHEAD * CH :], 3, c, 0, EARLY[c] * CH)
+            gather(slot(RING + c * EARLY, EARLY), 3, c, 0, EARLY * CH)
 
         o_codes = keep.tile([P, J], U32, name="o_codes", align_bytes=64)
         o_sc = keep.tile([P, J], U8, name="o_sc", align_bytes=64)
@@ -127,67 +138,91 @@ def tile_list_span_noneP_kernel(tc, xT, wgt, w_words, w_scales, offs, out_0, out
         def place(q, t):
             return last_b[:, t - 2, :] if q == NCH - 1 and t >= 2 else accs[q][:, t, :]
 
-        def front(q):
-            x_codes = keep.tile([P, PICKS * CH], U32, name=f"x_codes{q}", align_bytes=64)
-            x_sc = keep.tile([P, PICKS * CH], U8, name=f"x_sc{q}", align_bytes=64)
+        def pick_plane(piece, i):
+            q, c = divmod(piece, PICKS)
+            gather(slot(slots_of(piece)[i - 2]), i, c, q * CH, CH)
 
-            def project(c, t, start, stop):
+        def round_piece(piece):
+            q, c = divmod(piece, PICKS)
+            s2, s3 = slots_of(piece)
+            src = slot(s2, s3 - s2 + 1).rearrange("p (s j) -> p j s", j=CH)[:, :, :: s3 - s2]
+            if piece == PIECES - 1:
+                nc.vector.tensor_copy(out=packed[q][:, c, :, 2:4], in_=src)
+            else:
+                nc.scalar.copy(out=packed[q][:, c, :, 2:4], in_=src)
+
+        def project(piece):
+            q, c = divmod(piece, PICKS)
+            x_codes = keep.tile([P, CH], U32, name=f"x_codes{piece}", align_bytes=64)
+            x_sc = keep.tile([P, CH], U8, name=f"x_sc{piece}", align_bytes=64)
+            nc.vector.quantize_mx(out=x_codes[:].bitcast(FP8X4), scales=x_sc[:], in_=packed[q][:, c].rearrange("p j i -> p (j i)"))
+            width = 2 if q == NCH - 1 else PACK
+            for t in range(PACK):
                 nc.tensor.matmul_mx(
                     out=place(q, t),
                     lhsT=w_codes[:, 2 * P * t : 2 * P * (t + 1)].bitcast(FP4X4),
                     lhsT_scale=w_sc[:, P * t : P * (t + 1)],
-                    rhs=x_codes[:, c * CH : (c + 1) * CH].bitcast(FP8X4),
-                    rhs_scale=x_sc[:, c * CH : (c + 1) * CH],
-                    start=start,
-                    stop=stop,
+                    rhs=x_codes[:].bitcast(FP8X4),
+                    rhs_scale=x_sc[:],
+                    start=c == 0 and t % width == 0,
+                    stop=c == PICKS - 1 and t % width == width - 1,
                 )
 
-            for c in range(PICKS):
-                s2, s3 = q % AHEAD, AHEAD + q % EARLY[c]
-                if q >= EARLY[c]:
-                    gather(g23[c][:, s3 * CH : (s3 + 1) * CH], 3, c, q * CH, CH)
-                gather(g23[c][:, s2 * CH : (s2 + 1) * CH], 2, c, q * CH, CH)
-                src = g23[c][:, s2 * CH : (s3 + 1) * CH].rearrange("p (s j) -> p j s", j=CH)[:, :, :: s3 - s2]
-                if 2 * q + c in (7,):
-                    nc.vector.tensor_copy(out=packed[q][:, c, :, 2:4], in_=src)
-                else:
-                    nc.scalar.copy(out=packed[q][:, c, :, 2:4], in_=src)
-                pick = slice(c * CH, (c + 1) * CH)
-                nc.vector.quantize_mx(out=x_codes[:, pick].bitcast(FP8X4), scales=x_sc[:, pick], in_=packed[q][:, c].rearrange("p j i -> p (j i)"))
-                for t in range(PACK):
-                    width = 2 if q == NCH - 1 else PACK
-                    project(c, t, c == 0 and t % width == 0, c == PICKS - 1 and t % width == width - 1)
+        ys = [keep.tile([P, PACK, CH], F32, name=f"y{q}") for q in range(NCH)]
 
-        y_pairs = [keep.tile([P, 2 * CH, PACK], BF16, name=f"y_packed{h}", align_bytes=64) for h in range(2)]
-
-        def back(q):
-            cols = slice(q * CH, (q + 1) * CH)
-            y_packed = y_pairs[q // 2][:, (q % 2) * CH : (q % 2 + 1) * CH, :]
+        def empty(q):
             if q == NCH - 1:
-                y = keep.tile([P, PACK, CH], F32, name=f"y{q}")
                 for u, bank in enumerate((accs[q][:, 0:2, :], last_b[:])):
-                    nc.scalar.activation(out=y[:, 2 * u : 2 * u + 2, :], in_=bank, func=ABS)
-                    nc.vector.tensor_copy(out=y_packed[:, :, 2 * u : 2 * u + 2], in_=y[:, 2 * u : 2 * u + 2, :].rearrange("p t j -> p j t"))
-                nc.sync.dma_start(out=y_rows[:, :, cols], in_=y[:])
+                    nc.scalar.activation(out=ys[q][:, 2 * u : 2 * u + 2, :], in_=bank, func=ABS)
             else:
-                y = keep.tile([P, PACK, CH], F32, name=f"y{q}")
-                nc.scalar.activation(out=y[:], in_=accs[q][:], func=ABS)
-                nc.vector.tensor_copy(out=y_packed, in_=y[:].rearrange("p t j -> p j t"))
-                nc.sync.dma_start(out=y_rows[:, :, cols], in_=y[:])
-            if q == 1:
-                done = slice(0, 2 * CH)
-                nc.vector.quantize_mx(out=o_codes[:, done].bitcast(FP8X4), scales=o_sc[:, done], in_=y_pairs[0][:].rearrange("p j t -> p (j t)"))
-            if q >= 2:
-                nc.vector.quantize_mx(out=o_codes[:, cols].bitcast(FP8X4), scales=o_sc[:, cols], in_=y_packed.rearrange("p j t -> p (j t)"))
-            if q % 2 == 1:
-                done = slice((q - 1) * CH, (q + 1) * CH)
-                nc.sync.dma_start(out=o_words[:, done], in_=o_codes[:, done].bitcast(I32))
+                nc.scalar.activation(out=ys[q][:], in_=accs[q][:], func=ABS)
+            nc.sync.dma_start(out=y_rows[:, :, q * CH : (q + 1) * CH], in_=ys[q][:])
 
-        LAG = 2
-        for q in range(NCH + LAG):
-            if q < NCH:
-                front(q)
-            if q >= LAG:
-                back(q - LAG)
+        for piece in range(RING):
+            pick_plane(piece, 2)
+        for piece in range(PIECES - 2):
+            round_piece(piece)
+            if piece == 5:
+                pick_plane(7, 2)
+            project(piece)
+            if piece < 2:
+                pick_plane(piece + RING, 2)
+            if piece == 2:
+                pick_plane(6, 3)
+                pick_plane(6, 2)
+            if piece == 3:
+                pick_plane(7, 3)
+        empty(0)
+        round_piece(6)
+        round_piece(7)
+        project(6)
+        project(7)
+        for q in range(1, NCH):
+            empty(q)
+
+        y_packed = keep.tile([P, J, PACK], BF16, name="y_packed", tag="x0", align_bytes=64)
+
+        def round_y(q):
+            cols = slice(q * CH, (q + 1) * CH)
+            if q == NCH - 1:
+                for u in range(2):
+                    nc.vector.tensor_copy(out=y_packed[:, cols, 2 * u : 2 * u + 2], in_=ys[q][:, 2 * u : 2 * u + 2, :].rearrange("p t j -> p j t"))
+            else:
+                nc.vector.tensor_copy(out=y_packed[:, cols, :], in_=ys[q][:].rearrange("p t j -> p j t"))
+
+        def quantise_y(cols):
+            nc.vector.quantize_mx(out=o_codes[:, cols].bitcast(FP8X4), scales=o_sc[:, cols], in_=y_packed[:, cols, :].rearrange("p j t -> p (j t)"))
+
+        def store_words(cols):
+            nc.sync.dma_start(out=o_words[:, cols], in_=o_codes[:, cols].bitcast(I32))
+
+        for q in range(NCH - 1):
+            round_y(q)
+        quantise_y(slice(0, 2 * CH))
+        store_words(slice(0, 2 * CH))
+        round_y(NCH - 1)
+        quantise_y(slice(2 * CH, 3 * CH))
+        quantise_y(slice(3 * CH, 4 * CH))
+        store_words(slice(2 * CH, 4 * CH))
         for q in range(4):
             nc.sync.dma_start(out=out_2[0, 4 * q : 4 * q + 4, :].bitcast(I32), in_=o_sc[32 * q : 32 * q + 4, :].bitcast(I32))

@@ -146,7 +146,7 @@ def tile_list_span_noneP_kernel(tc, xT, wgt, w_words, w_scales, offs, out_0, out
             q, c = divmod(piece, PICKS)
             s2, s3 = slots_of(piece)
             src = slot(s2, s3 - s2 + 1).rearrange("p (s j) -> p j s", j=CH)[:, :, :: s3 - s2]
-            if piece == PIECES - 1:
+            if piece >= PIECES - 2:
                 nc.vector.tensor_copy(out=packed[q][:, c, :, 2:4], in_=src)
             else:
                 nc.scalar.copy(out=packed[q][:, c, :, 2:4], in_=src)
@@ -168,15 +168,16 @@ def tile_list_span_noneP_kernel(tc, xT, wgt, w_words, w_scales, offs, out_0, out
                     stop=c == PICKS - 1 and t % width == width - 1,
                 )
 
-        ys = [keep.tile([P, PACK, CH], F32, name=f"y{q}") for q in range(NCH)]
+        y_all = keep.tile([P, NCH, PACK, CH], F32, name="y_all")
+        ys = [y_all[:, q] for q in range(NCH)]
 
         def empty(q):
             if q == NCH - 1:
                 for u, bank in enumerate((accs[q][:, 0:2, :], last_b[:])):
                     nc.scalar.activation(out=ys[q][:, 2 * u : 2 * u + 2, :], in_=bank, func=ABS)
             else:
-                nc.scalar.activation(out=ys[q][:], in_=accs[q][:], func=ABS)
-            nc.sync.dma_start(out=y_rows[:, :, q * CH : (q + 1) * CH], in_=ys[q][:])
+                nc.scalar.activation(out=ys[q], in_=accs[q][:], func=ABS)
+            nc.sync.dma_start(out=y_rows[:, :, q * CH : (q + 1) * CH], in_=ys[q])
 
         for piece in range(RING):
             pick_plane(piece, 2)
@@ -208,7 +209,7 @@ def tile_list_span_noneP_kernel(tc, xT, wgt, w_words, w_scales, offs, out_0, out
                 for u in range(2):
                     nc.vector.tensor_copy(out=y_packed[:, cols, 2 * u : 2 * u + 2], in_=ys[q][:, 2 * u : 2 * u + 2, :].rearrange("p t j -> p j t"))
             else:
-                nc.vector.tensor_copy(out=y_packed[:, cols, :], in_=ys[q][:].rearrange("p t j -> p j t"))
+                nc.vector.tensor_copy(out=y_packed[:, cols, :].rearrange("p (c i) t -> p c t i", i=4), in_=ys[q].rearrange("p t (c i) -> p c t i", i=4))
 
         def quantise_y(cols):
             nc.vector.quantize_mx(out=o_codes[:, cols].bitcast(FP8X4), scales=o_sc[:, cols], in_=y_packed[:, cols, :].rearrange("p j t -> p (j t)"))
@@ -216,8 +217,11 @@ def tile_list_span_noneP_kernel(tc, xT, wgt, w_words, w_scales, offs, out_0, out
         def store_words(cols):
             nc.sync.dma_start(out=o_words[:, cols], in_=o_codes[:, cols].bitcast(I32))
 
-        for q in range(NCH - 1):
-            round_y(q)
+        nc.vector.tensor_copy(
+            out=y_packed[:, : 2 * CH, :].rearrange("p (q c i) t -> p q c t i", q=2, i=4),
+            in_=y_all[:, 0:2].rearrange("p q t (c i) -> p q c t i", i=4),
+        )
+        round_y(2)
         quantise_y(slice(0, 2 * CH))
         store_words(slice(0, 2 * CH))
         round_y(NCH - 1)

@@ -21,9 +21,16 @@ ABS = mybir.ActivationFunctionType.Abs
 P = 128
 PACK = 4
 PICKS = 2
+HEADS = 8
+GROUP = 16
 CH = 128
 NCH = J // CH
-LIST_ROWS = 16
+PIECES = PICKS * NCH
+HALF = J // 2
+QUADS = 4
+RING = 4
+EARLY = 3
+ON_VECTOR = 2
 
 
 def tile_list_span_noneP_kernel(tc, xT, wgt, w_words, w_scales, offs, out_0, out_1, out_2):
@@ -32,47 +39,46 @@ def tile_list_span_noneP_kernel(tc, xT, wgt, w_words, w_scales, offs, out_0, out
         keep = ctx.enter_context(tc.tile_pool(name="keep", bufs=1))
         psum = ctx.enter_context(tc.psum_pool(name="psum", bufs=1))
 
-        HALF = J // 2
         ws_raw = keep.tile([P, N], U8, name="ws_raw", tag="ws_raw", align_bytes=64)
         nc.gpsimd.memset(ws_raw[:].bitcast(I32), 0)
         ident = keep.tile([P, P], F32, name="ident")
         make_identity(nc, ident[:])
-        offsets = keep.tile([P, PICKS * J // LIST_ROWS], U16, name="offsets")
+        offsets = keep.tile([P, PICKS * J // GROUP], U16, name="offsets")
 
         w_raw = keep.tile([P, 2 * N], U8, name="w_raw", align_bytes=64)
         x_rows = xT.rearrange("(p i) t -> p i t", i=PACK)
         signed = keep.tile([P, PICKS * J], F32, name="signed")
-        xs = {i: keep.tile([P, T], F32, name=f"x{i}", tag=f"x{i}", align_bytes=64) for i in (0, 1)}
+        planes = {i: keep.tile([P, T], F32, name=f"x{i}", tag=f"x{i}", align_bytes=64) for i in (0, 1)}
         few = keep.tile([P, P], F32, name="few")
         nc.gpsimd.memset(few[P // 2 :, :], 0.0)
-        nc.sync.dma_start(out=few[: P // 2, :], in_=wgt.rearrange("(q e) (b u) -> q e b u", e=16, u=P)[:, 0])
+        nc.sync.dma_start(out=few[: P // 2, :], in_=wgt.rearrange("(g e) (b u) -> g e b u", e=GROUP, u=P)[:, 0])
         nc.sync.dma_start(out=w_raw[:].bitcast(I32), in_=w_words[0].bitcast(I32))
-        nc.sync.dma_start(out=ws_raw[0:16, :].bitcast(I32), in_=w_scales[0].bitcast(I32))
-        nc.sync.dma_start(out=xs[0][:], in_=x_rows[:, 0, :])
+        nc.sync.dma_start(out=ws_raw[0 : QUADS * 4, :].bitcast(I32), in_=w_scales[0].bitcast(I32))
+        nc.sync.dma_start(out=planes[0][:], in_=x_rows[:, 0, :])
         nc.sync.dma_start(offsets[:], offs)
-        nc.sync.dma_start(out=xs[1][:], in_=x_rows[:, 1, :])
+        nc.sync.dma_start(out=planes[1][:], in_=x_rows[:, 1, :])
 
         turned = psum.tile([P, P], F32, name="turned", tag="acc3")
         nc.tensor.transpose(turned[:], few[:], ident[:])
-        blocks = turned[:, : P // 2].rearrange("u (q b) -> u b q", b=8)
+        blocks = turned[:, : P // 2].rearrange("u (g b) -> u b g", g=HEADS)
         runs = ((3,), (0,), (1, 2))
-        for n, quarters in enumerate(runs):
-            spread = psum.tile([P, 2 * len(quarters), P], F32, name=f"spread{n}", tag=f"spread{n}")
+        for r, quarters in enumerate(runs):
+            spread = psum.tile([P, 2 * len(quarters), P], F32, name=f"spread{r}", tag=f"spread{r}")
             for m, v in enumerate(quarters):
                 wide = keep.tile([P, 2, P], F32, name=f"wide{v}", tag=f"wide{v}")
                 nc.scalar.activation(
-                    out=wide[:].rearrange("u b (q r) -> u b q r", r=16),
-                    in_=blocks[:, 2 * v : 2 * v + 2, :].unsqueeze(3).to_broadcast([P, 2, 8, 16]),
+                    out=wide[:].rearrange("u b (g e) -> u b g e", e=GROUP),
+                    in_=blocks[:, 2 * v : 2 * v + 2, :].unsqueeze(3).to_broadcast([P, 2, HEADS, GROUP]),
                     func=COPY,
-                    scale=1.0 if v >= 2 else -1.0,
+                    scale=1.0 if v * HALF >= J else -1.0,
                 )
                 for b in range(2):
                     nc.tensor.transpose(spread[:, 2 * m + b, :], wide[:, b, :], ident[:])
-            cols = slice(quarters[0] * HALF, (quarters[-1] + 1) * HALF)
-            if n == 0:
-                nc.vector.tensor_copy(out=signed[:, cols], in_=spread[:].rearrange("p b u -> p (b u)"))
+            entries = slice(quarters[0] * HALF, (quarters[-1] + 1) * HALF)
+            if r == 0:
+                nc.vector.tensor_copy(out=signed[:, entries], in_=spread[:].rearrange("p b u -> p (b u)"))
             else:
-                nc.scalar.copy(out=signed[:, cols], in_=spread[:].rearrange("p b u -> p (b u)"))
+                nc.scalar.copy(out=signed[:, entries], in_=spread[:].rearrange("p b u -> p (b u)"))
 
         w_codes = keep.tile([P, 2 * N], U8, name="w_codes", align_bytes=64)
         w_sc = keep.tile([P, N], U8, name="w_sc", align_bytes=64)
@@ -84,23 +90,23 @@ def tile_list_span_noneP_kernel(tc, xT, wgt, w_words, w_scales, offs, out_0, out
             out=w_sc[:].rearrange("p (t m) -> p t m", t=PACK),
             in_=ws_raw[:].rearrange("p (m t) -> p t m", t=PACK),
         )
-        for q in range(1, 4):
-            nc.sync.dma_start(out=w_sc[32 * q : 32 * q + 4, :].bitcast(I32), in_=w_sc[4 * q : 4 * q + 4, :].bitcast(I32))
-        xs[3] = keep.tile([P, T], F32, name="x3", tag="ws_raw", align_bytes=64)
-        xs[2] = keep.tile([P, T], F32, name="x2", tag="wide2")
+        for a in range(1, QUADS):
+            nc.sync.dma_start(out=w_sc[32 * a : 32 * a + 4, :].bitcast(I32), in_=w_sc[4 * a : 4 * a + 4, :].bitcast(I32))
+        planes[3] = keep.tile([P, T], F32, name="x3", tag="ws_raw", align_bytes=64)
+        planes[2] = keep.tile([P, T], F32, name="x2", tag="wide2")
         for i in (3, 2):
-            nc.sync.dma_start(out=xs[i][:], in_=x_rows[:, i, :])
+            nc.sync.dma_start(out=planes[i][:], in_=x_rows[:, i, :])
 
-        def gather(dst, i, c, j0, width):
-            a = c * J + j0
-            nc.vector.tensor_tensor(dst, xs[i][:].indirect(offsets[:, a // LIST_ROWS : (a + width) // LIST_ROWS]), signed[:, a : a + width], MULT)
+        def gather(dst, i, first, count):
+            picked = planes[i][:].indirect(offsets[:, first // GROUP : (first + count) // GROUP])
+            nc.vector.tensor_tensor(dst, picked, signed[:, first : first + count], MULT)
 
         g01 = keep.tile([P, 2, PICKS * J], F32, name="g01")
         for quarters in runs:
-            a, width = quarters[0] * HALF, len(quarters) * HALF
-            gather(g01[:, 0, a : a + width], 0, 0, a, width)
+            first, count = quarters[0] * HALF, len(quarters) * HALF
+            gather(g01[:, 0, first : first + count], 0, first, count)
         for c in range(PICKS):
-            gather(g01[:, 1, c * J : (c + 1) * J], 1, c, 0, J)
+            gather(g01[:, 1, c * J : (c + 1) * J], 1, c * J, J)
 
         halves = [keep.tile([P, PICKS, HALF, PACK], BF16, name=f"packed{h}", align_bytes=64) for h in range(2)]
         packed = [halves[q // 2][:, :, (q % 2) * CH : (q % 2 + 1) * CH, :] for q in range(NCH)]
@@ -108,24 +114,24 @@ def tile_list_span_noneP_kernel(tc, xT, wgt, w_words, w_scales, offs, out_0, out
             for h in range(2):
                 nc.scalar.copy(out=halves[h][:, c, :, 0:2], in_=g01[:, :, c * J + h * HALF : c * J + (h + 1) * HALF].rearrange("p i j -> p j i"))
 
-        PIECES = PICKS * NCH
-        RING = 4
-        EARLY = 3
         slots = keep.tile([P, (RING + PICKS * EARLY) * CH], F32, name="slots", tag="x0", align_bytes=64)
 
         def slot(s, count=1):
             return slots[:, s * CH : (s + count) * CH]
 
-        def slots_of(piece):
+        where = {}
+        for piece in range(PIECES):
             q, c = divmod(piece, PICKS)
-            if piece == PIECES - 1:
-                return 1, RING + c * EARLY + 1
-            if q >= EARLY:
-                return piece % RING, RING + c * EARLY + 1
-            return piece % RING, RING + c * EARLY + q
+            if piece < RING:
+                where[piece, 2] = piece
+            if q < EARLY:
+                where[piece, 3] = RING + c * EARLY + q
+        late = [(piece, i) for piece in range(RING, PIECES) for i in (3, 2) if (piece, i) not in where]
+        for n, (piece, i) in enumerate(late):
+            where[piece, i] = where[n, i]
 
         for c in range(PICKS):
-            gather(slot(RING + c * EARLY, EARLY), 3, c, 0, EARLY * CH)
+            gather(slot(RING + c * EARLY, EARLY), 3, c * J, EARLY * CH)
 
         o_codes = keep.tile([P, J], U32, name="o_codes", align_bytes=64)
         o_sc = keep.tile([P, J], U8, name="o_sc", align_bytes=64)
@@ -140,13 +146,13 @@ def tile_list_span_noneP_kernel(tc, xT, wgt, w_words, w_scales, offs, out_0, out
 
         def pick_plane(piece, i):
             q, c = divmod(piece, PICKS)
-            gather(slot(slots_of(piece)[i - 2]), i, c, q * CH, CH)
+            gather(slot(where[piece, i]), i, c * J + q * CH, CH)
 
         def round_piece(piece):
             q, c = divmod(piece, PICKS)
-            s2, s3 = slots_of(piece)
+            s2, s3 = where[piece, 2], where[piece, 3]
             src = slot(s2, s3 - s2 + 1).rearrange("p (s j) -> p j s", j=CH)[:, :, :: s3 - s2]
-            if piece >= PIECES - 2:
+            if piece >= PIECES - ON_VECTOR:
                 nc.vector.tensor_copy(out=packed[q][:, c, :, 2:4], in_=src)
             else:
                 nc.scalar.copy(out=packed[q][:, c, :, 2:4], in_=src)
@@ -156,7 +162,7 @@ def tile_list_span_noneP_kernel(tc, xT, wgt, w_words, w_scales, offs, out_0, out
             x_codes = keep.tile([P, CH], U32, name=f"x_codes{piece}", align_bytes=64)
             x_sc = keep.tile([P, CH], U8, name=f"x_sc{piece}", align_bytes=64)
             nc.vector.quantize_mx(out=x_codes[:].bitcast(FP8X4), scales=x_sc[:], in_=packed[q][:, c].rearrange("p j i -> p (j i)"))
-            width = 2 if q == NCH - 1 else PACK
+            in_bank = 2 if q == NCH - 1 else PACK
             for t in range(PACK):
                 nc.tensor.matmul_mx(
                     out=place(q, t),
@@ -164,52 +170,35 @@ def tile_list_span_noneP_kernel(tc, xT, wgt, w_words, w_scales, offs, out_0, out
                     lhsT_scale=w_sc[:, P * t : P * (t + 1)],
                     rhs=x_codes[:].bitcast(FP8X4),
                     rhs_scale=x_sc[:],
-                    start=c == 0 and t % width == 0,
-                    stop=c == PICKS - 1 and t % width == width - 1,
+                    start=c == 0 and t % in_bank == 0,
+                    stop=c == PICKS - 1 and t % in_bank == in_bank - 1,
                 )
 
         y_all = keep.tile([P, NCH, PACK, CH], F32, name="y_all")
-        ys = [y_all[:, q] for q in range(NCH)]
 
         def empty(q):
             if q == NCH - 1:
                 for u, bank in enumerate((accs[q][:, 0:2, :], last_b[:])):
-                    nc.scalar.activation(out=ys[q][:, 2 * u : 2 * u + 2, :], in_=bank, func=ABS)
+                    nc.scalar.activation(out=y_all[:, q][:, 2 * u : 2 * u + 2, :], in_=bank, func=ABS)
             else:
-                nc.scalar.activation(out=ys[q], in_=accs[q][:], func=ABS)
-            nc.sync.dma_start(out=y_rows[:, :, q * CH : (q + 1) * CH], in_=ys[q])
+                nc.scalar.activation(out=y_all[:, q], in_=accs[q][:], func=ABS)
+            nc.sync.dma_start(out=y_rows[:, :, q * CH : (q + 1) * CH], in_=y_all[:, q])
 
         for piece in range(RING):
             pick_plane(piece, 2)
-        for piece in range(PIECES - 2):
+        for piece in range(PIECES - ON_VECTOR):
             round_piece(piece)
-            if piece == 5:
-                pick_plane(7, 2)
             project(piece)
-            if piece < 2:
-                pick_plane(piece + RING, 2)
-            if piece == 2:
-                pick_plane(6, 3)
-                pick_plane(6, 2)
-            if piece == 3:
-                pick_plane(7, 3)
+            pick_plane(*late[piece])
         empty(0)
-        round_piece(6)
-        round_piece(7)
-        project(6)
-        project(7)
+        for piece in range(PIECES - ON_VECTOR, PIECES):
+            round_piece(piece)
+        for piece in range(PIECES - ON_VECTOR, PIECES):
+            project(piece)
         for q in range(1, NCH):
             empty(q)
 
         y_packed = keep.tile([P, J, PACK], BF16, name="y_packed", tag="x0", align_bytes=64)
-
-        def round_y(q):
-            cols = slice(q * CH, (q + 1) * CH)
-            if q == NCH - 1:
-                for u in range(2):
-                    nc.vector.tensor_copy(out=y_packed[:, cols, 2 * u : 2 * u + 2], in_=ys[q][:, 2 * u : 2 * u + 2, :].rearrange("p t j -> p j t"))
-            else:
-                nc.vector.tensor_copy(out=y_packed[:, cols, :].rearrange("p (c i) t -> p c t i", i=4), in_=ys[q].rearrange("p t (c i) -> p c t i", i=4))
 
         def quantise_y(cols):
             nc.vector.quantize_mx(out=o_codes[:, cols].bitcast(FP8X4), scales=o_sc[:, cols], in_=y_packed[:, cols, :].rearrange("p j t -> p (j t)"))
@@ -217,16 +206,21 @@ def tile_list_span_noneP_kernel(tc, xT, wgt, w_words, w_scales, offs, out_0, out
         def store_words(cols):
             nc.sync.dma_start(out=o_words[:, cols], in_=o_codes[:, cols].bitcast(I32))
 
+        chunk2, chunk3 = slice(2 * CH, 3 * CH), slice(3 * CH, J)
         nc.vector.tensor_copy(
-            out=y_packed[:, : 2 * CH, :].rearrange("p (q c i) t -> p q c t i", q=2, i=4),
-            in_=y_all[:, 0:2].rearrange("p q t (c i) -> p q c t i", i=4),
+            out=y_packed[:, :HALF, :].rearrange("p (q f e) t -> p q f t e", q=2, e=4),
+            in_=y_all[:, 0:2].rearrange("p q t (f e) -> p q f t e", e=4),
         )
-        round_y(2)
-        quantise_y(slice(0, 2 * CH))
-        store_words(slice(0, 2 * CH))
-        round_y(NCH - 1)
-        quantise_y(slice(2 * CH, 3 * CH))
-        quantise_y(slice(3 * CH, 4 * CH))
-        store_words(slice(2 * CH, 4 * CH))
-        for q in range(4):
-            nc.sync.dma_start(out=out_2[0, 4 * q : 4 * q + 4, :].bitcast(I32), in_=o_sc[32 * q : 32 * q + 4, :].bitcast(I32))
+        nc.vector.tensor_copy(
+            out=y_packed[:, chunk2, :].rearrange("p (f e) t -> p f t e", e=4),
+            in_=y_all[:, 2].rearrange("p t (f e) -> p f t e", e=4),
+        )
+        quantise_y(slice(0, HALF))
+        store_words(slice(0, HALF))
+        for u in range(2):
+            nc.vector.tensor_copy(out=y_packed[:, chunk3, 2 * u : 2 * u + 2], in_=y_all[:, 3][:, 2 * u : 2 * u + 2, :].rearrange("p t j -> p j t"))
+        quantise_y(chunk2)
+        quantise_y(chunk3)
+        store_words(slice(HALF, J))
+        for a in range(QUADS):
+            nc.sync.dma_start(out=out_2[0, 4 * a : 4 * a + 4, :].bitcast(I32), in_=o_sc[32 * a : 32 * a + 4, :].bitcast(I32))

@@ -26,11 +26,11 @@ GROUP = 16
 CH = 128
 NCH = J // CH
 PIECES = PICKS * NCH
-HALF = J // 2
+QUARTER = PICKS * J // 4
 QUADS = 4
 RING = 4
-EARLY = 3
-ON_VECTOR = 2
+ON_VECTOR = 1
+EARLY = 6
 
 
 def tile_list_span_noneP_kernel(tc, xT, wgt, w_words, w_scales, offs, out_0, out_1, out_2):
@@ -39,25 +39,35 @@ def tile_list_span_noneP_kernel(tc, xT, wgt, w_words, w_scales, offs, out_0, out
         keep = ctx.enter_context(tc.tile_pool(name="keep", bufs=1))
         psum = ctx.enter_context(tc.psum_pool(name="psum", bufs=1))
 
-        ws_raw = keep.tile([P, N], U8, name="ws_raw", tag="ws_raw", align_bytes=64)
-        nc.gpsimd.memset(ws_raw[:].bitcast(I32), 0)
-        ident = keep.tile([P, P], F32, name="ident")
-        make_identity(nc, ident[:])
         offsets = keep.tile([P, PICKS * J // GROUP], U16, name="offsets")
-
+        ws_raw = keep.tile([P, N], U8, name="ws_raw", align_bytes=64)
         w_raw = keep.tile([P, 2 * N], U8, name="w_raw", align_bytes=64)
-        x_rows = xT.rearrange("(p i) t -> p i t", i=PACK)
-        signed = keep.tile([P, PICKS * J], F32, name="signed")
-        planes = {i: keep.tile([P, T], F32, name=f"x{i}", tag=f"x{i}", align_bytes=64) for i in (0, 1)}
         few = keep.tile([P, P], F32, name="few")
+        ident = keep.tile([P, P], F32, name="ident")
+        planes = [keep.tile([P, T], F32, name=f"x{i}", tag=f"x{i}", align_bytes=64) for i in range(PACK)]
+        x_rows = xT.rearrange("(p i) t -> p i t", i=PACK)
+
+        nc.gpsimd.memset(ws_raw[:].bitcast(I32), 0)
+        make_identity(nc, ident[:])
         nc.gpsimd.memset(few[P // 2 :, :], 0.0)
+
         nc.sync.dma_start(out=few[: P // 2, :], in_=wgt.rearrange("(g e) (b u) -> g e b u", e=GROUP, u=P)[:, 0])
         nc.sync.dma_start(out=w_raw[:].bitcast(I32), in_=w_words[0].bitcast(I32))
         nc.sync.dma_start(out=ws_raw[0 : QUADS * 4, :].bitcast(I32), in_=w_scales[0].bitcast(I32))
         nc.sync.dma_start(out=planes[0][:], in_=x_rows[:, 0, :])
         nc.sync.dma_start(offsets[:], offs)
-        nc.sync.dma_start(out=planes[1][:], in_=x_rows[:, 1, :])
+        for i in (1, 3, 2):
+            nc.sync.dma_start(out=planes[i][:], in_=x_rows[:, i, :])
 
+        w_sc = keep.tile([P, N], U8, name="w_sc", align_bytes=64)
+        nc.vector.tensor_copy(
+            out=w_sc[:].rearrange("p (t m) -> p t m", t=PACK),
+            in_=ws_raw[:].rearrange("p (m t) -> p t m", t=PACK),
+        )
+        for a in range(1, QUADS):
+            nc.sync.dma_start(out=w_sc[32 * a : 32 * a + 4, :].bitcast(I32), in_=w_sc[4 * a : 4 * a + 4, :].bitcast(I32))
+
+        signed = keep.tile([P, PICKS * J], F32, name="signed")
         turned = psum.tile([P, P], F32, name="turned", tag="acc3")
         nc.tensor.transpose(turned[:], few[:], ident[:])
         blocks = turned[:, : P // 2].rearrange("u (g b) -> u b g", g=HEADS)
@@ -65,37 +75,26 @@ def tile_list_span_noneP_kernel(tc, xT, wgt, w_words, w_scales, offs, out_0, out
         for r, quarters in enumerate(runs):
             spread = psum.tile([P, 2 * len(quarters), P], F32, name=f"spread{r}", tag=f"spread{r}")
             for m, v in enumerate(quarters):
-                wide = keep.tile([P, 2, P], F32, name=f"wide{v}", tag=f"wide{v}")
+                wide = keep.tile([P, 2, P], F32, name=f"wide{v}", tag=f"wide{v}", align_bytes=64)
                 nc.scalar.activation(
                     out=wide[:].rearrange("u b (g e) -> u b g e", e=GROUP),
                     in_=blocks[:, 2 * v : 2 * v + 2, :].unsqueeze(3).to_broadcast([P, 2, HEADS, GROUP]),
                     func=COPY,
-                    scale=1.0 if v * HALF >= J else -1.0,
+                    scale=1.0 if v * QUARTER >= J else -1.0,
                 )
                 for b in range(2):
                     nc.tensor.transpose(spread[:, 2 * m + b, :], wide[:, b, :], ident[:])
-            entries = slice(quarters[0] * HALF, (quarters[-1] + 1) * HALF)
+            entries = slice(quarters[0] * QUARTER, (quarters[-1] + 1) * QUARTER)
             if r == 0:
                 nc.vector.tensor_copy(out=signed[:, entries], in_=spread[:].rearrange("p b u -> p (b u)"))
             else:
                 nc.scalar.copy(out=signed[:, entries], in_=spread[:].rearrange("p b u -> p (b u)"))
 
-        w_codes = keep.tile([P, 2 * N], U8, name="w_codes", align_bytes=64)
-        w_sc = keep.tile([P, N], U8, name="w_sc", align_bytes=64)
-        nc.vector.tensor_copy(
+        w_codes = keep.tile([P, 2 * N], U8, name="w_codes", tag="wide2", align_bytes=64)
+        nc.scalar.copy(
             out=w_codes[:].bitcast(U16).rearrange("p (t m) -> p t m", t=PACK),
             in_=w_raw[:].bitcast(U16).rearrange("p (m t) -> p t m", t=PACK),
         )
-        nc.vector.tensor_copy(
-            out=w_sc[:].rearrange("p (t m) -> p t m", t=PACK),
-            in_=ws_raw[:].rearrange("p (m t) -> p t m", t=PACK),
-        )
-        for a in range(1, QUADS):
-            nc.sync.dma_start(out=w_sc[32 * a : 32 * a + 4, :].bitcast(I32), in_=w_sc[4 * a : 4 * a + 4, :].bitcast(I32))
-        planes[3] = keep.tile([P, T], F32, name="x3", tag="ws_raw", align_bytes=64)
-        planes[2] = keep.tile([P, T], F32, name="x2", tag="wide2")
-        for i in (3, 2):
-            nc.sync.dma_start(out=planes[i][:], in_=x_rows[:, i, :])
 
         def gather(dst, i, first, count):
             picked = planes[i][:].indirect(offsets[:, first // GROUP : (first + count) // GROUP])
@@ -103,41 +102,42 @@ def tile_list_span_noneP_kernel(tc, xT, wgt, w_words, w_scales, offs, out_0, out
 
         g01 = keep.tile([P, 2, PICKS * J], F32, name="g01")
         for quarters in runs:
-            first, count = quarters[0] * HALF, len(quarters) * HALF
+            first, count = quarters[0] * QUARTER, len(quarters) * QUARTER
             gather(g01[:, 0, first : first + count], 0, first, count)
-        for c in range(PICKS):
+        for c in (1, 0):
             gather(g01[:, 1, c * J : (c + 1) * J], 1, c * J, J)
 
-        halves = [keep.tile([P, PICKS, HALF, PACK], BF16, name=f"packed{h}", align_bytes=64) for h in range(2)]
+        halves = [keep.tile([P, PICKS, QUARTER, PACK], BF16, name=f"packed{h}", align_bytes=64) for h in range(2)]
         packed = [halves[q // 2][:, :, (q % 2) * CH : (q % 2 + 1) * CH, :] for q in range(NCH)]
-        for c in range(PICKS):
-            for h in range(2):
-                nc.scalar.copy(out=halves[h][:, c, :, 0:2], in_=g01[:, :, c * J + h * HALF : c * J + (h + 1) * HALF].rearrange("p i j -> p j i"))
+        for v in (2, 3, 0, 1):
+            c, h = divmod(v, 2)
+            nc.scalar.copy(out=halves[h][:, c, :, 0:2], in_=g01[:, :, v * QUARTER : (v + 1) * QUARTER].rearrange("p i j -> p j i"))
 
-        slots = keep.tile([P, (RING + PICKS * EARLY) * CH], F32, name="slots", tag="x0", align_bytes=64)
+        slots = keep.tile([P, (RING + EARLY) * CH], F32, name="slots", tag="x0", align_bytes=64)
 
         def slot(s, count=1):
             return slots[:, s * CH : (s + count) * CH]
 
+        early = [(EARLY + 1 - c) // PICKS for c in range(PICKS)]
         where = {}
         for piece in range(PIECES):
             q, c = divmod(piece, PICKS)
             if piece < RING:
                 where[piece, 2] = piece
-            if q < EARLY:
-                where[piece, 3] = RING + c * EARLY + q
+            if piece < EARLY:
+                where[piece, 3] = RING + c * early[0] + q
         late = [(piece, i) for piece in range(RING, PIECES) for i in (3, 2) if (piece, i) not in where]
+        behind = (0, 1, 2, 3, 3, 4)
         for n, (piece, i) in enumerate(late):
-            where[piece, i] = where[n, i]
+            where[piece, i] = where[behind[n], i]
 
         for c in range(PICKS):
-            gather(slot(RING + c * EARLY, EARLY), 3, c * J, EARLY * CH)
+            gather(slot(RING + c * early[0], early[c]), 3, c * J, early[c] * CH)
 
         o_codes = keep.tile([P, J], U32, name="o_codes", align_bytes=64)
         o_sc = keep.tile([P, J], U8, name="o_sc", align_bytes=64)
         y_rows = out_0.rearrange("(p t) j -> p t j", t=PACK)
         o_words = out_1[0].rearrange("p j i -> p (j i)").bitcast(I32)
-
         accs = [psum.tile([P, PACK, CH], F32, name=f"acc{q}", tag=f"acc{q}") for q in range(NCH)]
         last_b = psum.tile([P, 2, CH], F32, name="last_b", tag="spread0")
 
@@ -186,14 +186,16 @@ def tile_list_span_noneP_kernel(tc, xT, wgt, w_words, w_scales, offs, out_0, out
 
         for piece in range(RING):
             pick_plane(piece, 2)
-        for piece in range(PIECES - ON_VECTOR):
+        for piece in range(PIECES - 2):
             round_piece(piece)
             project(piece)
-            pick_plane(*late[piece])
+            for n in range(len(late)):
+                if behind[n] == piece:
+                    pick_plane(*late[n])
         empty(0)
-        for piece in range(PIECES - ON_VECTOR, PIECES):
+        for piece in range(PIECES - 2, PIECES):
             round_piece(piece)
-        for piece in range(PIECES - ON_VECTOR, PIECES):
+        for piece in range(PIECES - 2, PIECES):
             project(piece)
         for q in range(1, NCH):
             empty(q)
@@ -208,19 +210,20 @@ def tile_list_span_noneP_kernel(tc, xT, wgt, w_words, w_scales, offs, out_0, out
 
         chunk2, chunk3 = slice(2 * CH, 3 * CH), slice(3 * CH, J)
         nc.vector.tensor_copy(
-            out=y_packed[:, :HALF, :].rearrange("p (q f e) t -> p q f t e", q=2, e=4),
+            out=y_packed[:, : 2 * CH, :].rearrange("p (q f e) t -> p q f t e", q=2, e=4),
             in_=y_all[:, 0:2].rearrange("p q t (f e) -> p q f t e", e=4),
         )
         nc.vector.tensor_copy(
             out=y_packed[:, chunk2, :].rearrange("p (f e) t -> p f t e", e=4),
             in_=y_all[:, 2].rearrange("p t (f e) -> p f t e", e=4),
         )
-        quantise_y(slice(0, HALF))
-        store_words(slice(0, HALF))
+        quantise_y(slice(0, 2 * CH))
+        store_words(slice(0, 2 * CH))
         for u in range(2):
             nc.vector.tensor_copy(out=y_packed[:, chunk3, 2 * u : 2 * u + 2], in_=y_all[:, 3][:, 2 * u : 2 * u + 2, :].rearrange("p t j -> p j t"))
         quantise_y(chunk2)
         quantise_y(chunk3)
-        store_words(slice(HALF, J))
+        store_words(slice(2 * CH, J))
         for a in range(QUADS):
-            nc.sync.dma_start(out=out_2[0, 4 * a : 4 * a + 4, :].bitcast(I32), in_=o_sc[32 * a : 32 * a + 4, :].bitcast(I32))
+            queue = nc.sync if a < 2 else nc.scalar
+            queue.dma_start(out=out_2[0, 4 * a : 4 * a + 4, :].bitcast(I32), in_=o_sc[32 * a : 32 * a + 4, :].bitcast(I32))

@@ -47,15 +47,15 @@ def tile_list_span_noneP_kernel(tc, xT, wgt, w_words, w_scales, offs, out_0, out
         planes = [keep.tile([P, T], F32, name=f"x{i}", tag=f"x{i}", align_bytes=64) for i in range(PACK)]
         x_rows = xT.rearrange("(p i) t -> p i t", i=PACK)
 
-        nc.gpsimd.memset(ws_raw[:].bitcast(I32), 0)
+        nc.gpsimd.memset(ws_raw[: P - 16, :].bitcast(I32), 0)
         make_identity(nc, ident[:])
         nc.gpsimd.memset(few[P // 2 :, :], 0.0)
 
         nc.sync.dma_start(out=few[: P // 2, :], in_=wgt.rearrange("(g e) (b u) -> g e b u", e=GROUP, u=P)[:, 0])
-        nc.sync.dma_start(out=w_raw[:].bitcast(I32), in_=w_words[0].bitcast(I32))
-        nc.sync.dma_start(out=ws_raw[0 : QUADS * 4, :].bitcast(I32), in_=w_scales[0].bitcast(I32))
+        nc.sync.dma_start(out=ws_raw[P - 16 :, :].bitcast(I32), in_=w_scales[0].bitcast(I32))
         nc.sync.dma_start(out=planes[0][:], in_=x_rows[:, 0, :])
         nc.sync.dma_start(offsets[:], offs)
+        nc.sync.dma_start(out=w_raw[:].bitcast(I32), in_=w_words[0].bitcast(I32))
         for i in (1, 3, 2):
             nc.sync.dma_start(out=planes[i][:], in_=x_rows[:, i, :])
 
@@ -64,33 +64,34 @@ def tile_list_span_noneP_kernel(tc, xT, wgt, w_words, w_scales, offs, out_0, out
             out=w_sc[:].rearrange("p (t m) -> p t m", t=PACK),
             in_=ws_raw[:].rearrange("p (m t) -> p t m", t=PACK),
         )
-        for a in range(1, QUADS):
-            nc.sync.dma_start(out=w_sc[32 * a : 32 * a + 4, :].bitcast(I32), in_=w_sc[4 * a : 4 * a + 4, :].bitcast(I32))
+        for a in range(QUADS):
+            nc.sync.dma_start(out=w_sc[32 * a : 32 * a + 4, :].bitcast(I32), in_=w_sc[P - 16 + 4 * a : P - 12 + 4 * a, :].bitcast(I32))
 
         signed = keep.tile([P, PICKS * J], F32, name="signed")
         turned = psum.tile([P, P], F32, name="turned", tag="acc3")
         nc.tensor.transpose(turned[:], few[:], ident[:])
         blocks = turned[:, : P // 2].rearrange("u (g b) -> u b g", g=HEADS)
-        runs = ((3,), (0,), (1, 2))
-        for r, quarters in enumerate(runs):
-            spread = psum.tile([P, 2 * len(quarters), P], F32, name=f"spread{r}", tag=f"spread{r}")
-            for m, v in enumerate(quarters):
-                wide = keep.tile([P, 2, P], F32, name=f"wide{v}", tag=f"wide{v}", align_bytes=64)
+        runs = (((7, 1),), ((5, 2),), ((0, 2),), ((2, 2), (4, 1)))
+        for r, parts in enumerate(runs):
+            first, count = parts[0][0], sum(n for b, n in parts)
+            spread = psum.tile([P, count, P], F32, name=f"spread{r}", tag=("spread0", "spread1", "spread2", "acc2")[r])
+            for b0, n in parts:
+                wide = keep.tile([P, n, P], F32, name=f"wide{b0}", tag=f"wide{b0}", align_bytes=64)
                 nc.scalar.activation(
                     out=wide[:].rearrange("u b (g e) -> u b g e", e=GROUP),
-                    in_=blocks[:, 2 * v : 2 * v + 2, :].unsqueeze(3).to_broadcast([P, 2, HEADS, GROUP]),
+                    in_=blocks[:, b0 : b0 + n, :].unsqueeze(3).to_broadcast([P, n, HEADS, GROUP]),
                     func=COPY,
-                    scale=1.0 if v * QUARTER >= J else -1.0,
+                    scale=1.0 if b0 * P >= J else -1.0,
                 )
-                for b in range(2):
-                    nc.tensor.transpose(spread[:, 2 * m + b, :], wide[:, b, :], ident[:])
-            entries = slice(quarters[0] * QUARTER, (quarters[-1] + 1) * QUARTER)
+                for b in range(n):
+                    nc.tensor.transpose(spread[:, b0 - first + b, :], wide[:, b, :], ident[:])
+            entries = slice(first * P, (first + count) * P)
             if r == 0:
                 nc.vector.tensor_copy(out=signed[:, entries], in_=spread[:].rearrange("p b u -> p (b u)"))
             else:
                 nc.scalar.copy(out=signed[:, entries], in_=spread[:].rearrange("p b u -> p (b u)"))
 
-        w_codes = keep.tile([P, 2 * N], U8, name="w_codes", tag="wide2", align_bytes=64)
+        w_codes = keep.tile([P, 2 * N], U8, name="w_codes", tag="wide4", align_bytes=64)
         nc.scalar.copy(
             out=w_codes[:].bitcast(U16).rearrange("p (t m) -> p t m", t=PACK),
             in_=w_raw[:].bitcast(U16).rearrange("p (m t) -> p t m", t=PACK),
@@ -101,9 +102,8 @@ def tile_list_span_noneP_kernel(tc, xT, wgt, w_words, w_scales, offs, out_0, out
             nc.vector.tensor_tensor(dst, picked, signed[:, first : first + count], MULT)
 
         g01 = keep.tile([P, 2, PICKS * J], F32, name="g01")
-        for quarters in runs:
-            first, count = quarters[0] * QUARTER, len(quarters) * QUARTER
-            gather(g01[:, 0, first : first + count], 0, first, count)
+        for first, count in ((7, 1), (5, 2), (0, 2), (2, 3)):
+            gather(g01[:, 0, first * P : (first + count) * P], 0, first * P, count * P)
         for c in (1, 0):
             gather(g01[:, 1, c * J : (c + 1) * J], 1, c * J, J)
 

@@ -29,7 +29,7 @@ PIECES = PICKS * NCH
 QUARTER = PICKS * J // 4
 QUADS = 4
 RING = 4
-ON_VECTOR = 1
+ON_VECTOR = 2
 EARLY = 6
 
 
@@ -104,12 +104,12 @@ def tile_list_span_noneP_kernel(tc, xT, wgt, w_words, w_scales, offs, out_0, out
         g01 = keep.tile([P, 2, PICKS * J], F32, name="g01")
         for first, count in ((7, 1), (5, 2), (0, 2), (2, 3)):
             gather(g01[:, 0, first * P : (first + count) * P], 0, first * P, count * P)
-        for c in (1, 0):
+        for c in range(PICKS):
             gather(g01[:, 1, c * J : (c + 1) * J], 1, c * J, J)
 
         halves = [keep.tile([P, PICKS, QUARTER, PACK], BF16, name=f"packed{h}", align_bytes=64) for h in range(2)]
         packed = [halves[q // 2][:, :, (q % 2) * CH : (q % 2 + 1) * CH, :] for q in range(NCH)]
-        for v in (2, 3, 0, 1):
+        for v in range(4):
             c, h = divmod(v, 2)
             nc.scalar.copy(out=halves[h][:, c, :, 0:2], in_=g01[:, :, v * QUARTER : (v + 1) * QUARTER].rearrange("p i j -> p j i"))
 
@@ -127,7 +127,7 @@ def tile_list_span_noneP_kernel(tc, xT, wgt, w_words, w_scales, offs, out_0, out
             if piece < EARLY:
                 where[piece, 3] = RING + c * early[0] + q
         late = [(piece, i) for piece in range(RING, PIECES) for i in (3, 2) if (piece, i) not in where]
-        behind = (0, 1, 2, 3, 3, 4)
+        behind = (0, 1, 2, 3, 4, 5)
         for n, (piece, i) in enumerate(late):
             where[piece, i] = where[behind[n], i]
 
@@ -225,5 +225,4 @@ def tile_list_span_noneP_kernel(tc, xT, wgt, w_words, w_scales, offs, out_0, out
         quantise_y(chunk3)
         store_words(slice(2 * CH, J))
         for a in range(QUADS):
-            queue = nc.sync if a < 2 else nc.scalar
-            queue.dma_start(out=out_2[0, 4 * a : 4 * a + 4, :].bitcast(I32), in_=o_sc[32 * a : 32 * a + 4, :].bitcast(I32))
+            nc.sync.dma_start(out=out_2[0, 4 * a : 4 * a + 4, :].bitcast(I32), in_=o_sc[32 * a : 32 * a + 4, :].bitcast(I32))

@@ -29,7 +29,7 @@ PIECES = PICKS * NCH
 QUARTER = PICKS * J // 4
 QUADS = 4
 RING = 4
-ON_VECTOR = 2
+ON_VECTOR = 1
 EARLY = 6
 
 
@@ -55,8 +55,9 @@ def tile_list_span_noneP_kernel(tc, xT, wgt, w_words, w_scales, offs, out_0, out
         nc.sync.dma_start(out=ws_raw[P - 16 :, :].bitcast(I32), in_=w_scales[0].bitcast(I32))
         nc.sync.dma_start(out=planes[0][:], in_=x_rows[:, 0, :])
         nc.sync.dma_start(offsets[:], offs)
+        nc.sync.dma_start(out=planes[1][:], in_=x_rows[:, 1, :])
         nc.sync.dma_start(out=w_raw[:].bitcast(I32), in_=w_words[0].bitcast(I32))
-        for i in (1, 3, 2):
+        for i in (3, 2):
             nc.sync.dma_start(out=planes[i][:], in_=x_rows[:, i, :])
 
         w_sc = keep.tile([P, N], U8, name="w_sc", align_bytes=64)
@@ -127,7 +128,7 @@ def tile_list_span_noneP_kernel(tc, xT, wgt, w_words, w_scales, offs, out_0, out
             if piece < EARLY:
                 where[piece, 3] = RING + c * early[0] + q
         late = [(piece, i) for piece in range(RING, PIECES) for i in (3, 2) if (piece, i) not in where]
-        behind = (0, 1, 2, 3, 4, 5)
+        behind = (0, 1, 2, 3, 3, 4)
         for n, (piece, i) in enumerate(late):
             where[piece, i] = where[behind[n], i]
 

@@ -51,7 +51,7 @@ def tile_list_span_noneP_kernel(tc, xT, wgt, w_words, w_scales, offs, out_0, out
         make_identity(nc, ident[:])
         nc.gpsimd.memset(few[P // 2 :, :], 0.0)
 
-        nc.sync.dma_start(out=few[: P // 2, :], in_=wgt.rearrange("(g e) (b u) -> g e b u", e=GROUP, u=P)[:, 0])
+        nc.sync.dma_start(out=few[: P // 2, :], in_=wgt.rearrange("r (h b u) -> (r h) b u", h=2, u=P)[:: GROUP + 1])
         nc.sync.dma_start(out=ws_raw[P - 16 :, :].bitcast(I32), in_=w_scales[0].bitcast(I32))
         nc.sync.dma_start(out=planes[0][:], in_=x_rows[:, 0, :])
         nc.sync.dma_start(offsets[:], offs)

@@ -226,4 +226,5 @@ def tile_list_span_noneP_kernel(tc, xT, wgt, w_words, w_scales, offs, out_0, out
         quantise_y(chunk3)
         store_words(slice(2 * CH, J))
         for a in range(QUADS):
-            nc.sync.dma_start(out=out_2[0, 4 * a : 4 * a + 4, :].bitcast(I32), in_=o_sc[32 * a : 32 * a + 4, :].bitcast(I32))
+            queue = nc.sync if a < QUADS - 1 else nc.scalar
+            queue.dma_start(out=out_2[0, 4 * a : 4 * a + 4, :].bitcast(I32), in_=o_sc[32 * a : 32 * a + 4, :].bitcast(I32))

@@ -28,9 +28,10 @@ NCH = J // CH
 PIECES = PICKS * NCH
 QUARTER = PICKS * J // 4
 QUADS = 4
+SCALE_ROWS = 4 * QUADS
 RING = 4
-ON_VECTOR = 1
-EARLY = 6
+EARLY = 3
+LEAD = T // 4
 
 
 def tile_list_span_noneP_kernel(tc, xT, wgt, w_words, w_scales, offs, out_0, out_1, out_2):
@@ -47,13 +48,14 @@ def tile_list_span_noneP_kernel(tc, xT, wgt, w_words, w_scales, offs, out_0, out
         planes = [keep.tile([P, T], F32, name=f"x{i}", tag=f"x{i}", align_bytes=64) for i in range(PACK)]
         x_rows = xT.rearrange("(p i) t -> p i t", i=PACK)
 
-        nc.gpsimd.memset(ws_raw[: P - 16, :].bitcast(I32), 0)
+        nc.gpsimd.memset(ws_raw[: P - SCALE_ROWS, :].bitcast(I32), 0)
         make_identity(nc, ident[:])
         nc.gpsimd.memset(few[P // 2 :, :], 0.0)
 
         nc.sync.dma_start(out=few[: P // 2, :], in_=wgt.rearrange("r (h b u) -> (r h) b u", h=2, u=P)[:: GROUP + 1])
-        nc.sync.dma_start(out=ws_raw[P - 16 :, :].bitcast(I32), in_=w_scales[0].bitcast(I32))
-        nc.sync.dma_start(out=planes[0][:], in_=x_rows[:, 0, :])
+        nc.sync.dma_start(out=planes[0][:, :LEAD], in_=x_rows[:, 0, :LEAD])
+        nc.sync.dma_start(out=ws_raw[P - SCALE_ROWS :, :].bitcast(I32), in_=w_scales[0].bitcast(I32))
+        nc.sync.dma_start(out=planes[0][:, LEAD:], in_=x_rows[:, 0, LEAD:])
         nc.sync.dma_start(offsets[:], offs)
         nc.sync.dma_start(out=planes[1][:], in_=x_rows[:, 1, :])
         nc.sync.dma_start(out=w_raw[:].bitcast(I32), in_=w_words[0].bitcast(I32))
@@ -66,21 +68,23 @@ def tile_list_span_noneP_kernel(tc, xT, wgt, w_words, w_scales, offs, out_0, out
             in_=ws_raw[:].rearrange("p (m t) -> p t m", t=PACK),
         )
         for a in range(QUADS):
-            nc.sync.dma_start(out=w_sc[32 * a : 32 * a + 4, :].bitcast(I32), in_=w_sc[P - 16 + 4 * a : P - 12 + 4 * a, :].bitcast(I32))
+            row = P - SCALE_ROWS + 4 * a
+            nc.sync.dma_start(out=w_sc[32 * a : 32 * a + 4, :].bitcast(I32), in_=w_sc[row : row + 4, :].bitcast(I32))
 
         signed = keep.tile([P, PICKS * J], F32, name="signed")
         turned = psum.tile([P, P], F32, name="turned", tag="acc3")
         nc.tensor.transpose(turned[:], few[:], ident[:])
-        blocks = turned[:, : P // 2].rearrange("u (g b) -> u b g", g=HEADS)
+        strips = turned[:, : P // 2].rearrange("u (g b) -> u b g", g=HEADS)
         runs = (((7, 1),), ((5, 2),), ((0, 2),), ((2, 2), (4, 1)))
+        spans = [(parts[0][0], sum(n for b0, n in parts)) for parts in runs]
         for r, parts in enumerate(runs):
-            first, count = parts[0][0], sum(n for b, n in parts)
+            first, count = spans[r]
             spread = psum.tile([P, count, P], F32, name=f"spread{r}", tag=("spread0", "spread1", "spread2", "acc2")[r])
             for b0, n in parts:
                 wide = keep.tile([P, n, P], F32, name=f"wide{b0}", tag=f"wide{b0}", align_bytes=64)
                 nc.scalar.activation(
                     out=wide[:].rearrange("u b (g e) -> u b g e", e=GROUP),
-                    in_=blocks[:, b0 : b0 + n, :].unsqueeze(3).to_broadcast([P, n, HEADS, GROUP]),
+                    in_=strips[:, b0 : b0 + n, :].unsqueeze(3).to_broadcast([P, n, HEADS, GROUP]),
                     func=COPY,
                     scale=1.0 if b0 * P >= J else -1.0,
                 )
@@ -103,7 +107,7 @@ def tile_list_span_noneP_kernel(tc, xT, wgt, w_words, w_scales, offs, out_0, out
             nc.vector.tensor_tensor(dst, picked, signed[:, first : first + count], MULT)
 
         g01 = keep.tile([P, 2, PICKS * J], F32, name="g01")
-        for first, count in ((7, 1), (5, 2), (0, 2), (2, 3)):
+        for first, count in spans:
             gather(g01[:, 0, first * P : (first + count) * P], 0, first * P, count * P)
         for c in range(PICKS):
             gather(g01[:, 1, c * J : (c + 1) * J], 1, c * J, J)
@@ -114,31 +118,31 @@ def tile_list_span_noneP_kernel(tc, xT, wgt, w_words, w_scales, offs, out_0, out
             c, h = divmod(v, 2)
             nc.scalar.copy(out=halves[h][:, c, :, 0:2], in_=g01[:, :, v * QUARTER : (v + 1) * QUARTER].rearrange("p i j -> p j i"))
 
-        slots = keep.tile([P, (RING + EARLY) * CH], F32, name="slots", tag="x0", align_bytes=64)
+        slots = keep.tile([P, (RING + PICKS * EARLY) * CH], F32, name="slots", tag="x0", align_bytes=64)
 
         def slot(s, count=1):
             return slots[:, s * CH : (s + count) * CH]
 
-        early = [(EARLY + 1 - c) // PICKS for c in range(PICKS)]
         where = {}
         for piece in range(PIECES):
             q, c = divmod(piece, PICKS)
             if piece < RING:
                 where[piece, 2] = piece
-            if piece < EARLY:
-                where[piece, 3] = RING + c * early[0] + q
+            if q < EARLY:
+                where[piece, 3] = RING + c * EARLY + q
         late = [(piece, i) for piece in range(RING, PIECES) for i in (3, 2) if (piece, i) not in where]
         behind = (0, 1, 2, 3, 3, 4)
         for n, (piece, i) in enumerate(late):
             where[piece, i] = where[behind[n], i]
 
         for c in range(PICKS):
-            gather(slot(RING + c * early[0], early[c]), 3, c * J, early[c] * CH)
+            gather(slot(RING + c * EARLY, EARLY), 3, c * J, EARLY * CH)
 
         o_codes = keep.tile([P, J], U32, name="o_codes", align_bytes=64)
         o_sc = keep.tile([P, J], U8, name="o_sc", align_bytes=64)
         y_rows = out_0.rearrange("(p t) j -> p t j", t=PACK)
         o_words = out_1[0].rearrange("p j i -> p (j i)").bitcast(I32)
+
         accs = [psum.tile([P, PACK, CH], F32, name=f"acc{q}", tag=f"acc{q}") for q in range(NCH)]
         last_b = psum.tile([P, 2, CH], F32, name="last_b", tag="spread0")
 
@@ -153,7 +157,7 @@ def tile_list_span_noneP_kernel(tc, xT, wgt, w_words, w_scales, offs, out_0, out
             q, c = divmod(piece, PICKS)
             s2, s3 = where[piece, 2], where[piece, 3]
             src = slot(s2, s3 - s2 + 1).rearrange("p (s j) -> p j s", j=CH)[:, :, :: s3 - s2]
-            if piece >= PIECES - ON_VECTOR:
+            if piece == PIECES - 1:
                 nc.vector.tensor_copy(out=packed[q][:, c, :, 2:4], in_=src)
             else:
                 nc.scalar.copy(out=packed[q][:, c, :, 2:4], in_=src)
@@ -187,16 +191,16 @@ def tile_list_span_noneP_kernel(tc, xT, wgt, w_words, w_scales, offs, out_0, out
 
         for piece in range(RING):
             pick_plane(piece, 2)
-        for piece in range(PIECES - 2):
+        for piece in range(PIECES - PICKS):
             round_piece(piece)
             project(piece)
             for n in range(len(late)):
                 if behind[n] == piece:
                     pick_plane(*late[n])
         empty(0)
-        for piece in range(PIECES - 2, PIECES):
+        for piece in range(PIECES - PICKS, PIECES):
             round_piece(piece)
-        for piece in range(PIECES - 2, PIECES):
+        for piece in range(PIECES - PICKS, PIECES):
             project(piece)
         for q in range(1, NCH):
             empty(q)

from contextlib import ExitStack

import concourse.mybir as mybir
from concourse.masks import make_identity

K, N, T, J = 512, 512, 2048, 512
FLOPS = 2 * 2 * K * N * J

F32 = mybir.dt.float32
BF16 = mybir.dt.bfloat16
I32 = mybir.dt.int32
U32 = mybir.dt.uint32
U16 = mybir.dt.uint16
U8 = mybir.dt.uint8
FP8X4 = mybir.dt.float8_e4m3fn_x4
FP4X4 = mybir.dt.float4_e2m1fn_x4
MULT = mybir.AluOpType.mult
COPY = mybir.ActivationFunctionType.Copy
ABS = mybir.ActivationFunctionType.Abs

P = 128
PACK = 4
PICKS = 2
HEADS = 8
GROUP = 16
CH = 128
NCH = J // CH
PIECES = PICKS * NCH
QUARTER = PICKS * J // 4
QUADS = 4
SCALE_ROWS = 4 * QUADS
RING = 4
EARLY = 3
LEAD = T // 4


def tile_list_span_noneP_kernel(tc, xT, wgt, w_words, w_scales, offs, out_0, out_1, out_2):
    nc = tc.nc
    with ExitStack() as ctx:
        keep = ctx.enter_context(tc.tile_pool(name="keep", bufs=1))
        psum = ctx.enter_context(tc.psum_pool(name="psum", bufs=1))

        offsets = keep.tile([P, PICKS * J // GROUP], U16, name="offsets")
        ws_raw = keep.tile([P, N], U8, name="ws_raw", align_bytes=64)
        w_raw = keep.tile([P, 2 * N], U8, name="w_raw", align_bytes=64)
        few = keep.tile([P, P], F32, name="few")
        ident = keep.tile([P, P], F32, name="ident")
        planes = [keep.tile([P, T], F32, name=f"x{i}", tag=f"x{i}", align_bytes=64) for i in range(PACK)]
        x_rows = xT.rearrange("(p i) t -> p i t", i=PACK)

        nc.gpsimd.memset(ws_raw[: P - SCALE_ROWS, :].bitcast(I32), 0)
        make_identity(nc, ident[:])
        nc.gpsimd.memset(few[P // 2 :, :], 0.0)

        nc.sync.dma_start(out=few[: P // 2, :], in_=wgt.rearrange("r (h b u) -> (r h) b u", h=2, u=P)[:: GROUP + 1])
        nc.sync.dma_start(out=planes[0][:, :LEAD], in_=x_rows[:, 0, :LEAD])
        nc.sync.dma_start(out=ws_raw[P - SCALE_ROWS :, :].bitcast(I32), in_=w_scales[0].bitcast(I32))
        nc.sync.dma_start(out=planes[0][:, LEAD:], in_=x_rows[:, 0, LEAD:])
        nc.sync.dma_start(offsets[:], offs)
        nc.sync.dma_start(out=planes[1][:], in_=x_rows[:, 1, :])
        nc.sync.dma_start(out=w_raw[:].bitcast(I32), in_=w_words[0].bitcast(I32))
        for i in (3, 2):
            nc.sync.dma_start(out=planes[i][:], in_=x_rows[:, i, :])

        w_sc = keep.tile([P, N], U8, name="w_sc", align_bytes=64)
        nc.vector.tensor_copy(
            out=w_sc[:].rearrange("p (t m) -> p t m", t=PACK),
            in_=ws_raw[:].rearrange("p (m t) -> p t m", t=PACK),
        )
        for a in range(QUADS):
            row = P - SCALE_ROWS + 4 * a
            nc.sync.dma_start(out=w_sc[32 * a : 32 * a + 4, :].bitcast(I32), in_=w_sc[row : row + 4, :].bitcast(I32))

        signed = keep.tile([P, PICKS * J], F32, name="signed")
        turned = psum.tile([P, P], F32, name="turned", tag="acc3")
        nc.tensor.transpose(turned[:], few[:], ident[:])
        strips = turned[:, : P // 2].rearrange("u (g b) -> u b g", g=HEADS)
        runs = (((7, 1),), ((5, 2),), ((0, 2),), ((2, 2), (4, 1)))
        spans = [(parts[0][0], sum(n for b0, n in parts)) for parts in runs]
        for r, parts in enumerate(runs):
            first, count = spans[r]
            spread = psum.tile([P, count, P], F32, name=f"spread{r}", tag=("spread0", "spread1", "spread2", "acc2")[r])
            for b0, n in parts:
                wide = keep.tile([P, n, P], F32, name=f"wide{b0}", tag=f"wide{b0}", align_bytes=64)
                nc.scalar.activation(
                    out=wide[:].rearrange("u b (g e) -> u b g e", e=GROUP),
                    in_=strips[:, b0 : b0 + n, :].unsqueeze(3).to_broadcast([P, n, HEADS, GROUP]),
                    func=COPY,
                    scale=1.0 if b0 * P >= J else -1.0,
                )
                for b in range(n):
                    nc.tensor.transpose(spread[:, b0 - first + b, :], wide[:, b, :], ident[:])
            entries = slice(first * P, (first + count) * P)
            if r == 0:
                nc.vector.tensor_copy(out=signed[:, entries], in_=spread[:].rearrange("p b u -> p (b u)"))
            else:
                nc.scalar.copy(out=signed[:, entries], in_=spread[:].rearrange("p b u -> p (b u)"))

        w_codes = keep.tile([P, 2 * N], U8, name="w_codes", tag="wide4", align_bytes=64)
        nc.scalar.copy(
            out=w_codes[:].bitcast(U16).rearrange("p (t m) -> p t m", t=PACK),
            in_=w_raw[:].bitcast(U16).rearrange("p (m t) -> p t m", t=PACK),
        )

        def gather(dst, i, first, count):
            picked = planes[i][:].indirect(offsets[:, first // GROUP : (first + count) // GROUP])
            nc.vector.tensor_tensor(dst, picked, signed[:, first : first + count], MULT)

        g01 = keep.tile([P, 2, PICKS * J], F32, name="g01")
        for first, count in spans:
            gather(g01[:, 0, first * P : (first + count) * P], 0, first * P, count * P)
        for c in range(PICKS):
            gather(g01[:, 1, c * J : (c + 1) * J], 1, c * J, J)

        halves = [keep.tile([P, PICKS, QUARTER, PACK], BF16, name=f"packed{h}", align_bytes=64) for h in range(2)]
        packed = [halves[q // 2][:, :, (q % 2) * CH : (q % 2 + 1) * CH, :] for q in range(NCH)]
        for v in range(4):
            c, h = divmod(v, 2)
            nc.scalar.copy(out=halves[h][:, c, :, 0:2], in_=g01[:, :, v * QUARTER : (v + 1) * QUARTER].rearrange("p i j -> p j i"))

        slots = keep.tile([P, (RING + PICKS * EARLY) * CH], F32, name="slots", tag="x0", align_bytes=64)

        def slot(s, count=1):
            return slots[:, s * CH : (s + count) * CH]

        where = {}
        for piece in range(PIECES):
            q, c = divmod(piece, PICKS)
            if piece < RING:
                where[piece, 2] = piece
            if q < EARLY:
                where[piece, 3] = RING + c * EARLY + q
        late = [(piece, i) for piece in range(RING, PIECES) for i in (3, 2) if (piece, i) not in where]
        behind = (0, 1, 2, 3, 3, 4)
        for n, (piece, i) in enumerate(late):
            where[piece, i] = where[behind[n], i]

        for c in range(PICKS):
            gather(slot(RING + c * EARLY, EARLY), 3, c * J, EARLY * CH)

        o_codes = keep.tile([P, J], U32, name="o_codes", align_bytes=64)
        o_sc = keep.tile([P, J], U8, name="o_sc", align_bytes=64)
        y_rows = out_0.rearrange("(p t) j -> p t j", t=PACK)
        o_words = out_1[0].rearrange("p j i -> p (j i)").bitcast(I32)

        accs = [psum.tile([P, PACK, CH], F32, name=f"acc{q}", tag=f"acc{q}") for q in range(NCH)]
        last_b = psum.tile([P, 2, CH], F32, name="last_b", tag="spread0")

        def place(q, t):
            return last_b[:, t - 2, :] if q == NCH - 1 and t >= 2 else accs[q][:, t, :]

        def pick_plane(piece, i):
            q, c = divmod(piece, PICKS)
            gather(slot(where[piece, i]), i, c * J + q * CH, CH)

        def round_piece(piece):
            q, c = divmod(piece, PICKS)
            s2, s3 = where[piece, 2], where[piece, 3]
            src = slot(s2, s3 - s2 + 1).rearrange("p (s j) -> p j s", j=CH)[:, :, :: s3 - s2]
            if piece == PIECES - 1:
                nc.vector.tensor_copy(out=packed[q][:, c, :, 2:4], in_=src)
            else:
                nc.scalar.copy(out=packed[q][:, c, :, 2:4], in_=src)

        def project(piece):
            q, c = divmod(piece, PICKS)
            x_codes = keep.tile([P, CH], U32, name=f"x_codes{piece}", align_bytes=64)
            x_sc = keep.tile([P, CH], U8, name=f"x_sc{piece}", align_bytes=64)
            nc.vector.quantize_mx(out=x_codes[:].bitcast(FP8X4), scales=x_sc[:], in_=packed[q][:, c].rearrange("p j i -> p (j i)"))
            in_bank = 2 if q == NCH - 1 else PACK
            for t in range(PACK):
                nc.tensor.matmul_mx(
                    out=place(q, t),
                    lhsT=w_codes[:, 2 * P * t : 2 * P * (t + 1)].bitcast(FP4X4),
                    lhsT_scale=w_sc[:, P * t : P * (t + 1)],
                    rhs=x_codes[:].bitcast(FP8X4),
                    rhs_scale=x_sc[:],
                    start=c == 0 and t % in_bank == 0,
                    stop=c == PICKS - 1 and t % in_bank == in_bank - 1,
                )

        y_all = keep.tile([P, NCH, PACK, CH], F32, name="y_all")

        def empty(q):
            if q == NCH - 1:
                for u, bank in enumerate((accs[q][:, 0:2, :], last_b[:])):
                    nc.scalar.activation(out=y_all[:, q][:, 2 * u : 2 * u + 2, :], in_=bank, func=ABS)
            else:
                nc.scalar.activation(out=y_all[:, q], in_=accs[q][:], func=ABS)
            nc.sync.dma_start(out=y_rows[:, :, q * CH : (q + 1) * CH], in_=y_all[:, q])

        for piece in range(RING):
            pick_plane(piece, 2)
        for piece in range(PIECES - PICKS):
            round_piece(piece)
            project(piece)
            for n in range(len(late)):
                if behind[n] == piece:
                    pick_plane(*late[n])
        empty(0)
        for piece in range(PIECES - PICKS, PIECES):
            round_piece(piece)
        for piece in range(PIECES - PICKS, PIECES):
            project(piece)
        for q in range(1, NCH):
            empty(q)

        y_packed = keep.tile([P, J, PACK], BF16, name="y_packed", tag="x0", align_bytes=64)

        def quantise_y(cols):
            nc.vector.quantize_mx(out=o_codes[:, cols].bitcast(FP8X4), scales=o_sc[:, cols], in_=y_packed[:, cols, :].rearrange("p j t -> p (j t)"))

        def store_words(cols):
            nc.sync.dma_start(out=o_words[:, cols], in_=o_codes[:, cols].bitcast(I32))

        chunk2, chunk3 = slice(2 * CH, 3 * CH), slice(3 * CH, J)
        nc.vector.tensor_copy(
            out=y_packed[:, : 2 * CH, :].rearrange("p (q f e) t -> p q f t e", q=2, e=4),
            in_=y_all[:, 0:2].rearrange("p q t (f e) -> p q f t e", e=4),
        )
        nc.vector.tensor_copy(
            out=y_packed[:, chunk2, :].rearrange("p (f e) t -> p f t e", e=4),
            in_=y_all[:, 2].rearrange("p t (f e) -> p f t e", e=4),
        )
        quantise_y(slice(0, 2 * CH))
        store_words(slice(0, 2 * CH))
        for u in range(2):
            nc.vector.tensor_copy(out=y_packed[:, chunk3, 2 * u : 2 * u + 2], in_=y_all[:, 3][:, 2 * u : 2 * u + 2, :].rearrange("p t j -> p j t"))
        quantise_y(chunk2)
        quantise_y(chunk3)
        store_words(slice(2 * CH, J))
        for a in range(QUADS):
            queue = nc.sync if a < QUADS - 1 else nc.scalar
            queue.dma_start(out=out_2[0, 4 * a : 4 * a + 4, :].bitcast(I32), in_=o_sc[32 * a : 32 * a + 4, :].bitcast(I32))
